import numpy as np
import ml_dtypes


def mxq(x, axis, fmt="e4m3"):
    dtype, down = {"e4m3": (ml_dtypes.float8_e4m3fn, 7), "e5m2": (ml_dtypes.float8_e5m2, 14)}[fmt]
    v = np.moveaxis(np.asarray(x, np.float32).astype(ml_dtypes.bfloat16).astype(np.float64), axis, -1)
    blocks = v.reshape(v.shape[:-1] + (-1, 32))
    amax = np.abs(blocks).max(-1, keepdims=True)
    byte = np.maximum(np.where(amax > 0, np.frexp(amax)[1] - 1 + 127, 0) - down, 1)
    scale = np.exp2(byte - 127.0)
    codes = (blocks / scale).astype(np.float32).astype(dtype).astype(np.float64)
    return np.moveaxis((codes * scale).reshape(v.shape), -1, axis)


WIDE = False


def mx_kscale(k):
    if not WIDE:
        return np.ones(k)
    levels = np.array([10, -10, 5, -5, 0])
    if k % 512:
        return np.exp2(np.random.permutation(np.resize(levels, k // 32))).repeat(32)
    a = np.empty((k // 512, 16))
    for p in range(k // 512):
        a[p, :8] = np.random.permutation(np.resize(levels, 8))
        for g in range(8):
            far = levels[np.abs(levels - a[p, g]) >= 10]
            a[p, g + 8] = far[np.random.randint(len(far))]
    return np.exp2(a.ravel()).repeat(32)


def f64(x):
    return np.asarray(x).astype(np.float64)


def striped(idx):
    return np.tile(idx.reshape(-1, 16).T, (8, 1)).astype(np.uint16)


def unstriped(offs):
    return offs[:16].T.reshape(-1).astype(np.int64)


E2M1 = np.array([0.0, 0.5, 1.0, 1.5, 2.0, 3.0, 4.0, 6.0, -0.0, -0.5, -1.0, -1.5, -2.0, -3.0, -4.0, -6.0])


def pack_weight(w, fmt):
    k, n = w.shape
    w = f64(np.asarray(w, np.float32).astype(ml_dtypes.bfloat16)).reshape(k // 32, 32, n)
    amax = np.abs(w).max(1)
    if fmt == "e4m3":
        byte = np.frexp(amax)[1] - 1 + 127 - 7
    else:
        mant, ex = np.frexp(amax / 6.0)
        byte = np.where(mant > 0.5, ex, ex - 1) + 127
    byte = np.clip(np.where(amax > 0, byte, 1), 1, 254)
    scaled = (w * np.exp2(127.0 - byte)[:, None, :]).reshape(k, n).astype(np.float32)
    by_word = np.ascontiguousarray(scaled.reshape(k // 512, 128, 4, n).transpose(0, 1, 3, 2))
    if fmt == "e4m3":
        words = by_word.astype(ml_dtypes.float8_e4m3fn).view(np.uint8)
    else:
        c = by_word.astype(ml_dtypes.float4_e2m1fn).view(np.uint8) & 0xF
        words = (c[..., 0::2] | (c[..., 1::2] << 4)).reshape(k // 512, 128, 2 * n)
    return np.ascontiguousarray(words), np.ascontiguousarray(byte.astype(np.uint8).reshape(k // 512, 16, n))


def unpack_weight(words, scales, fmt):
    g, _, n = scales.shape
    words = np.ascontiguousarray(words).reshape(g, 128, n, -1)
    if fmt == "e4m3":
        vals = words.view(ml_dtypes.float8_e4m3fn).astype(np.float64)
    else:
        nib = np.empty((g, 128, n, 4), np.uint8)
        nib[..., 0::2] = words & 0xF
        nib[..., 1::2] = words >> 4
        vals = E2M1[nib]
    vals = vals * np.repeat(np.exp2(scales.astype(np.float64) - 127.0), 8, axis=1)[..., None]
    return vals.transpose(0, 1, 3, 2).reshape(g * 512, n)


def gelu(v):
    return 0.5 * v * (1.0 + np.tanh(np.sqrt(2.0 / np.pi) * (v + 0.044715 * v**3)))


K, T, E, C, H, N = 512, 1536, 4, 256, 512, 128


def by_expert(wq, xq):
    return np.concatenate([wq[e].T @ xq[:, e * C:(e + 1) * C] for e in range(E)], axis=1)


def setup_inputs():
    n = np.random.standard_normal
    s = mx_kscale(K)[:, None]
    u = mx_kscale(H)
    w1 = [pack_weight(m, "e2m1") for m in n((E, K, H)) / np.sqrt(K) / s[None] * u[None, None, :]]
    w2 = [pack_weight(m, "e2m1") for m in n((E, H, N)) / np.sqrt(H) / u[None, :, None]]
    return {
        "xT": (n((K, T)) * s).astype(np.float32),
        "w1_words": np.stack([m[0] for m in w1]),
        "w1_scales": np.stack([m[1] for m in w1]),
        "w2_words": np.stack([m[0] for m in w2]),
        "w2_scales": np.stack([m[1] for m in w2]),
        "gate": np.tile(np.random.uniform(0.2, 1.0, E * C), (N, 1)).astype(np.float32),
        "offs": striped(np.random.permutation(T)[:E * C]),
        "dst": striped(np.random.permutation(T)[:E * C]),
    }


def reference(xT, w1_words, w1_scales, w2_words, w2_scales, gate, offs, dst):
    idx = unstriped(offs)
    w1 = np.stack([unpack_weight(w1_words[e], w1_scales[e], "e2m1") for e in range(E)])
    w2 = np.stack([unpack_weight(w2_words[e], w2_scales[e], "e2m1") for e in range(E)])
    xq = mxq(f64(xT)[:, idx], 0, "e4m3")
    h = gelu(by_expert(w1, xq))
    y = by_expert(w2, mxq(h, 0, "e4m3"))
    out = np.zeros((N, T))
    out[:, unstriped(dst)] = f64(gate) * y
    return out

@@ -1,0 +1,239 @@
+from contextlib import ExitStack
+
+import concourse.mybir as mybir
+
+F32 = mybir.dt.float32
+BF16 = mybir.dt.bfloat16
+I32 = mybir.dt.int32
+U32 = mybir.dt.uint32
+U16 = mybir.dt.uint16
+U8 = mybir.dt.uint8
+FP8X4 = mybir.dt.float8_e4m3fn_x4
+FP4X4 = mybir.dt.float4_e2m1fn_x4
+GELU = mybir.ActivationFunctionType.Gelu_apprx_tanh
+MULT = mybir.AluOpType.mult
+
+P = 128
+K, T, E, C, H, N = 512, 1536, 4, 256, 512, 128
+S = E * C
+FLOPS = 2 * S * (K * H + H * N)
+
+
+def tile_moe_two_mlp_gelu_kernel(tc, xT, w1_words, w1_scales, w2_words, w2_scales, gate, offs, dst, out):
+    nc = tc.nc
+    with ExitStack() as ctx:
+        keep = ctx.enter_context(tc.tile_pool(name="keep", bufs=1))
+        ps_a = ctx.enter_context(tc.psum_pool(name="ps_a", bufs=4))
+        ps_l = ctx.enter_context(tc.psum_pool(name="ps_l", bufs=1))
+        ps_y = ctx.enter_context(tc.psum_pool(name="ps_y", bufs=1))
+
+        offs_t = keep.tile([P, S // 16], U16, name="offs_t")
+        dst_t = keep.tile([P, S // 16], U16, name="dst_t")
+        w1_raw = keep.tile([P, E * 2 * H], U8, name="w1_raw", align_bytes=64)
+        w1_perm = keep.tile([P, E * 2 * H], U8, name="w1_perm", align_bytes=64)
+        s1_raw = keep.tile([P, E, H], U8, name="s1_raw", align_bytes=64)
+        s1_perm = keep.tile([P, E * H], U8, name="s1_perm", align_bytes=64)
+        w2_t = keep.tile([P, E, 2 * N], U8, name="w2_t", align_bytes=64)
+        s2_t = keep.tile([P, E, N], U8, name="s2_t", align_bytes=64)
+        gate_t = keep.tile([P, S], F32, name="gate_t")
+        placed = keep.tile([P, T], F32, name="placed")
+        warm = keep.tile([P, 1], F32, name="warm")
+
+        nc.gpsimd.memset(s1_raw[:].rearrange("p e i -> p (e i)").bitcast(I32), 0)
+        nc.vector.memset(warm[:], 0.0)
+        nc.scalar.activation(out=warm[:], in_=warm[:], func=GELU)
+        nc.gpsimd.memset(s2_t[:].rearrange("p e i -> p (e i)").bitcast(I32), 0)
+        nc.gpsimd.memset(placed[:], 0.0)
+
+        def load_w1(e0, e1):
+            nc.sync.dma_start(
+                out=w1_raw[:, 2 * H * e0 : 2 * H * e1].rearrange("p (e b) -> p e b", b=2 * H).bitcast(I32),
+                in_=w1_words[e0:e1, 0].rearrange("e p b -> p e b").bitcast(I32),
+            )
+
+        def load_late():
+            nc.sync.dma_start(
+                out=w2_t[:].bitcast(I32), in_=w2_words[:, 0].rearrange("e p b -> p e b").bitcast(I32)
+            )
+            for q in range(4):
+                nc.sync.dma_start(
+                    out=s2_t[32 * q : 32 * q + 4, :, :].bitcast(I32),
+                    in_=w2_scales[:, 0, 4 * q : 4 * q + 4, :].rearrange("e q i -> q e i").bitcast(I32),
+                )
+            nc.sync.dma_start(dst_t[:], dst)
+            nc.sync.dma_start(out=gate_t[:], in_=gate)
+
+        def permute_words(e0, e1):
+            nc.vector.tensor_copy(
+                out=w1_perm[:, 2 * H * e0 : 2 * H * e1].bitcast(U16).rearrange("p (e j m) -> p e j m", j=4, m=P),
+                in_=w1_raw[:, 2 * H * e0 : 2 * H * e1].bitcast(U16).rearrange("p (e m j) -> p e j m", j=4, m=P),
+            )
+
+        def permute_scales():
+            nc.vector.tensor_copy(
+                out=s1_perm[:].rearrange("p (e j m) -> p e j m", e=E, j=4),
+                in_=s1_raw[:].rearrange("p e (m j) -> p e j m", j=4),
+            )
+
+        pairs = [keep.tile([P, T, 2], BF16, name="pairs%d" % h, align_bytes=64) for h in range(2)]
+        grouped = keep.tile([P, S, 4], BF16, name="grouped", align_bytes=64)
+        x_rows = xT.rearrange("(p h j) t -> h p j t", h=2, j=2)
+        chunks = [[(0, 512), (512, 512), (1024, 512)], [(0, 512), (512, 512), (1024, 512)]]
+        x_raw = {}
+
+        def load_x(h, c):
+            t0, n = chunks[h][c]
+            x_raw[h, c] = keep.tile([P, 2, n], F32, name="x_raw%d_%d" % (h, c))
+            nc.sync.dma_start(out=x_raw[h, c][:], in_=x_rows[h, :, :, t0 : t0 + n])
+
+        load_x(0, 0)
+        for q in range(4):
+            nc.sync.dma_start(
+                out=s1_raw[32 * q : 32 * q + 4, :, :].bitcast(I32),
+                in_=w1_scales[:, 0, 4 * q : 4 * q + 4, :].rearrange("e q i -> q e i").bitcast(I32),
+            )
+        load_w1(0, 1)
+        nc.sync.dma_start(offs_t[:], offs)
+        for h, c in ((0, 1), (0, 2), (1, 0), (1, 1), (1, 2)):
+            load_x(h, c)
+        load_w1(1, 4)
+        load_late()
+
+        def pair(engine_copy, h, c, a, n):
+            t0 = chunks[h][c][0]
+            engine_copy(
+                out=pairs[h][:, t0 + a : t0 + a + n, :].rearrange("p (c i) j -> p c j i", i=4),
+                in_=x_raw[h, c][:, :, a : a + n].rearrange("p j (c i) -> p c j i", i=4),
+            )
+
+        sc, ve = nc.scalar.copy, nc.vector.tensor_copy
+        slot_words = grouped[:].rearrange("p s j -> p (s j)").bitcast(U32).rearrange("p (s h) -> p s h", h=2)
+
+        def pick(h, s0, n):
+            nc.vector.tensor_copy(
+                out=slot_words[:, s0 : s0 + n, h],
+                in_=pairs[h][:].rearrange("p t j -> p (t j)").bitcast(U32).indirect(offs_t[:, s0 // 16 : (s0 + n) // 16]),
+            )
+
+        def gather(e):
+            pick(1, C * e, C)
+
+        permute_words(0, 1)
+        permute_scales()
+        pair(sc, 0, 0, 0, 512)
+        pair(sc, 0, 1, 0, 512)
+        pair(sc, 0, 2, 0, 256)
+        pair(ve, 0, 2, 256, 256)
+        pick(0, 0, 1024)
+        pair(sc, 1, 0, 0, 512)
+        pair(sc, 1, 1, 0, 512)
+        pair(sc, 1, 2, 0, 192)
+        pair(ve, 1, 2, 192, 320)
+
+        x_codes, x_scales = {}, {}
+
+        def quant_x(e):
+            x_codes[e] = keep.tile([P, C], U32, name="x_codes%d" % e, align_bytes=64)
+            x_scales[e] = keep.tile([P, C], U8, name="x_scales%d" % e, align_bytes=64)
+            nc.vector.quantize_mx(
+                out=x_codes[e][:].bitcast(FP8X4),
+                scales=x_scales[e][:],
+                in_=grouped[:, C * e : C * (e + 1), :].rearrange("p s j -> p (s j)"),
+            )
+
+        acc_tags = {(3, 1): "h2", (2, 0): "s0", (3, 0): "s1"}
+        y_tags = {0: "s0", 1: "s1", 2: "h2"}
+        h_raw, h_codes, h_scales, y_raw, y_ps = {}, {}, {}, {}, {}
+
+        def layer1(e):
+            h_raw[e] = keep.tile([P, C, 4], BF16, name="h_raw%d" % e, align_bytes=64)
+            for b in range(2):
+                if (e, b) in acc_tags:
+                    acc = ps_l.tile([P, 4, 128], F32, name="acc_%d%d" % (e, b), tag=acc_tags[e, b])
+                else:
+                    acc = ps_a.tile([P, 4, 128], F32, name="acc")
+                for j in range(4):
+                    w0 = (e * 4 + j) * 128
+                    nc.tensor.matmul_mx(
+                        out=acc[:, j, :],
+                        lhsT=w1_perm[:, 2 * w0 : 2 * (w0 + 128)].bitcast(FP4X4),
+                        lhsT_scale=s1_perm[:, w0 : w0 + 128],
+                        rhs=x_codes[e][:, 128 * b : 128 * (b + 1)].bitcast(FP8X4),
+                        rhs_scale=x_scales[e][:, 128 * b : 128 * (b + 1)],
+                        start=True,
+                        stop=True,
+                    )
+                nc.scalar.activation(
+                    out=h_raw[e][:, 128 * b : 128 * (b + 1), :],
+                    in_=acc[:].rearrange("p j s -> p s j"),
+                    func=GELU,
+                )
+
+        def quant_h(e):
+            h_codes[e] = keep.tile([P, C], U32, name="h_codes%d" % e, align_bytes=64)
+            h_scales[e] = keep.tile([P, C], U8, name="h_scales%d" % e, align_bytes=64)
+            nc.vector.quantize_mx(
+                out=h_codes[e][:].bitcast(FP8X4),
+                scales=h_scales[e][:],
+                in_=h_raw[e][:].rearrange("p s j -> p (s j)"),
+            )
+
+        def layer2(e, gated=False):
+            if e in y_tags:
+                y_ps[e] = ps_l.tile([P, C], F32, name="y_ps%d" % e, tag=y_tags[e])
+            else:
+                y_ps[e] = ps_y.tile([P, C], F32, name="y_ps")
+            nc.tensor.matmul_mx(
+                out=y_ps[e][:],
+                lhsT=w2_t[:, e, :].bitcast(FP4X4),
+                lhsT_scale=s2_t[:, e, :],
+                rhs=h_codes[e][:].bitcast(FP8X4),
+                rhs_scale=h_scales[e][:],
+                start=True,
+                stop=True,
+            )
+            y_raw[e] = keep.tile([P, C], F32, name="y_raw%d" % e)
+            if gated:
+                nc.vector.tensor_tensor(y_raw[e][:], y_ps[e][:], gate_t[:, C * e : C * (e + 1)], MULT)
+            else:
+                nc.scalar.copy(out=y_raw[e][:], in_=y_ps[e][:])
+
+        def scatter(e, gated=False):
+            if gated:
+                nc.vector.tensor_copy(placed[:].indirect(dst_t[:, 16 * e : 16 * (e + 1)]), y_raw[e][:])
+                return
+            nc.vector.tensor_tensor(
+                placed[:].indirect(dst_t[:, 16 * e : 16 * (e + 1)]),
+                y_raw[e][:],
+                gate_t[:, C * e : C * (e + 1)],
+                MULT,
+            )
+
+        gather(0)
+        quant_x(0)
+        permute_words(1, 2)
+        layer1(0)
+        gather(1)
+        quant_x(1)
+        quant_h(0)
+        layer2(0)
+        layer1(1)
+        permute_words(2, 3)
+        gather(2)
+        scatter(0)
+        gather(3)
+        quant_x(2)
+        layer1(2)
+        quant_x(3)
+        quant_h(1)
+        permute_words(3, 4)
+        quant_h(2)
+        layer2(1)
+        layer1(3)
+        scatter(1)
+        layer2(2)
+        scatter(2)
+        quant_h(3)
+        layer2(3)
+        scatter(3)
+        nc.sync.dma_start(out=out, in_=placed[:])

@@ -23,19 +23,16 @@ def tile_moe_two_mlp_gelu_kernel(tc, xT, w1_words, w1_scales, w2_words, w2_scale
     nc = tc.nc
     with ExitStack() as ctx:
         keep = ctx.enter_context(tc.tile_pool(name="keep", bufs=1))
-        ps_a = ctx.enter_context(tc.psum_pool(name="ps_a", bufs=4))
-        ps_l = ctx.enter_context(tc.psum_pool(name="ps_l", bufs=1))
-        ps_y = ctx.enter_context(tc.psum_pool(name="ps_y", bufs=1))
+        shared = ctx.enter_context(tc.tile_pool(name="shared", bufs=1))
+        late = ctx.enter_context(tc.tile_pool(name="late", bufs=1))
+        ps_a = ctx.enter_context(tc.psum_pool(name="ps_a", bufs=6))
+        ps_y = ctx.enter_context(tc.psum_pool(name="ps_y", bufs=2))
 
         offs_t = keep.tile([P, S // 16], U16, name="offs_t")
         dst_t = keep.tile([P, S // 16], U16, name="dst_t")
-        w1_raw = keep.tile([P, E * 2 * H], U8, name="w1_raw", align_bytes=64)
-        w1_perm = keep.tile([P, E * 2 * H], U8, name="w1_perm", align_bytes=64)
         s1_raw = keep.tile([P, E, H], U8, name="s1_raw", align_bytes=64)
         s1_perm = keep.tile([P, E * H], U8, name="s1_perm", align_bytes=64)
-        w2_t = keep.tile([P, E, 2 * N], U8, name="w2_t", align_bytes=64)
         s2_t = keep.tile([P, E, N], U8, name="s2_t", align_bytes=64)
-        gate_t = keep.tile([P, S], F32, name="gate_t")
         placed = keep.tile([P, T], F32, name="placed")
         warm = keep.tile([P, 1], F32, name="warm")
 
@@ -45,59 +42,64 @@ def tile_moe_two_mlp_gelu_kernel(tc, xT, w1_words, w1_scales, w2_words, w2_scale
         nc.gpsimd.memset(s2_t[:].rearrange("p e i -> p (e i)").bitcast(I32), 0)
         nc.gpsimd.memset(placed[:], 0.0)
 
+        w1_raw, w1_perm = {}, {}
+
         def load_w1(e0, e1):
+            raw = keep.tile([P, (e1 - e0) * 2 * H], U8, name="w1_raw%d" % e0, align_bytes=64)
             nc.sync.dma_start(
-                out=w1_raw[:, 2 * H * e0 : 2 * H * e1].rearrange("p (e b) -> p e b", b=2 * H).bitcast(I32),
+                out=raw[:].rearrange("p (e b) -> p e b", b=2 * H).bitcast(I32),
                 in_=w1_words[e0:e1, 0].rearrange("e p b -> p e b").bitcast(I32),
             )
+            for e in range(e0, e1):
+                w1_raw[e] = raw[:, 2 * H * (e - e0) : 2 * H * (e - e0 + 1)]
 
-        def load_late():
-            nc.sync.dma_start(
-                out=w2_t[:].bitcast(I32), in_=w2_words[:, 0].rearrange("e p b -> p e b").bitcast(I32)
-            )
+        def load_scales(tile, scales):
             for q in range(4):
                 nc.sync.dma_start(
-                    out=s2_t[32 * q : 32 * q + 4, :, :].bitcast(I32),
-                    in_=w2_scales[:, 0, 4 * q : 4 * q + 4, :].rearrange("e q i -> q e i").bitcast(I32),
+                    out=tile[32 * q : 32 * q + 4, :, :].bitcast(I32),
+                    in_=scales[:, 0, 4 * q : 4 * q + 4, :].rearrange("e q i -> q e i").bitcast(I32),
                 )
-            nc.sync.dma_start(dst_t[:], dst)
-            nc.sync.dma_start(out=gate_t[:], in_=gate)
 
-        def permute_words(e0, e1):
+        def permute_words(e):
+            if e == 3:
+                w1_perm[e] = shared.tile([P, 2 * H], U8, name="w1_perm%d" % e, align_bytes=64, offset=0)
+            else:
+                w1_perm[e] = keep.tile([P, 2 * H], U8, name="w1_perm%d" % e, align_bytes=64)
             nc.vector.tensor_copy(
-                out=w1_perm[:, 2 * H * e0 : 2 * H * e1].bitcast(U16).rearrange("p (e j m) -> p e j m", j=4, m=P),
-                in_=w1_raw[:, 2 * H * e0 : 2 * H * e1].bitcast(U16).rearrange("p (e m j) -> p e j m", j=4, m=P),
+                out=w1_perm[e][:].bitcast(U16).rearrange("p (j c) -> p j c", j=4),
+                in_=w1_raw[e].bitcast(U16).rearrange("p (c j) -> p j c", j=4),
             )
 
         def permute_scales():
             nc.vector.tensor_copy(
-                out=s1_perm[:].rearrange("p (e j m) -> p e j m", e=E, j=4),
-                in_=s1_raw[:].rearrange("p e (m j) -> p e j m", j=4),
+                out=s1_perm[:].rearrange("p (j c) -> p j c", j=4),
+                in_=s1_raw[:].rearrange("p e (m j) -> p j (e m)", j=4),
             )
 
         pairs = [keep.tile([P, T, 2], BF16, name="pairs%d" % h, align_bytes=64) for h in range(2)]
         grouped = keep.tile([P, S, 4], BF16, name="grouped", align_bytes=64)
         x_rows = xT.rearrange("(p h j) t -> h p j t", h=2, j=2)
-        chunks = [[(0, 512), (512, 512), (1024, 512)], [(0, 512), (512, 512), (1024, 512)]]
+        chunks = [[(0, 1024), (1024, 512)], [(0, 512), (512, 512), (1024, 512)]]
         x_raw = {}
 
         def load_x(h, c):
             t0, n = chunks[h][c]
-            x_raw[h, c] = keep.tile([P, 2, n], F32, name="x_raw%d_%d" % (h, c))
+            if (h, c) == (1, 2):
+                x_raw[h, c] = late.tile([P, 2, n], F32, name="x_raw%d_%d" % (h, c), align_bytes=64, offset=0)
+            else:
+                x_raw[h, c] = keep.tile([P, 2, n], F32, name="x_raw%d_%d" % (h, c))
             nc.sync.dma_start(out=x_raw[h, c][:], in_=x_rows[h, :, :, t0 : t0 + n])
 
-        load_x(0, 0)
-        for q in range(4):
-            nc.sync.dma_start(
-                out=s1_raw[32 * q : 32 * q + 4, :, :].bitcast(I32),
-                in_=w1_scales[:, 0, 4 * q : 4 * q + 4, :].rearrange("e q i -> q e i").bitcast(I32),
-            )
-        load_w1(0, 1)
         nc.sync.dma_start(offs_t[:], offs)
-        for h, c in ((0, 1), (0, 2), (1, 0), (1, 1), (1, 2)):
+        load_w1(0, 1)
+        load_x(0, 0)
+        load_scales(s1_raw, w1_scales)
+        for h, c in ((0, 1), (1, 0), (1, 1), (1, 2)):
             load_x(h, c)
-        load_w1(1, 4)
-        load_late()
+        load_w1(1, 2)
+        load_w1(2, 4)
+        load_scales(s2_t, w2_scales)
+        nc.sync.dma_start(dst_t[:], dst)
 
         def pair(engine_copy, h, c, a, n):
             t0 = chunks[h][c][0]
@@ -115,51 +117,56 @@ def tile_moe_two_mlp_gelu_kernel(tc, xT, w1_words, w1_scales, w2_words, w2_scale
                 in_=pairs[h][:].rearrange("p t j -> p (t j)").bitcast(U32).indirect(offs_t[:, s0 // 16 : (s0 + n) // 16]),
             )
 
-        def gather(e):
-            pick(1, C * e, C)
-
-        permute_words(0, 1)
-        permute_scales()
+        permute_words(0)
         pair(sc, 0, 0, 0, 512)
-        pair(sc, 0, 1, 0, 512)
-        pair(sc, 0, 2, 0, 256)
-        pair(ve, 0, 2, 256, 256)
+        pair(ve, 0, 0, 512, 512)
+        permute_scales()
+        pair(sc, 0, 1, 0, 160)
+        pair(ve, 0, 1, 160, 352)
         pick(0, 0, 1024)
         pair(sc, 1, 0, 0, 512)
-        pair(sc, 1, 1, 0, 512)
-        pair(sc, 1, 2, 0, 192)
-        pair(ve, 1, 2, 192, 320)
+        pair(sc, 1, 1, 0, 256)
+        pair(ve, 1, 1, 256, 256)
+        pair(sc, 1, 2, 0, 160)
+        pair(ve, 1, 2, 160, 352)
+        w2_t = late.tile([P, E, 2 * N], U8, name="w2_t", align_bytes=64, offset=0)
+        gate_t = late.tile([P, S], F32, name="gate_t", align_bytes=64, offset=E * 2 * N)
+        nc.scalar.dma_start(out=w2_t[:].bitcast(I32), in_=w2_words[:, 0].rearrange("e p b -> p e b").bitcast(I32))
+        nc.scalar.dma_start(out=gate_t[:], in_=gate)
 
         x_codes, x_scales = {}, {}
-
-        def quant_x(e):
-            x_codes[e] = keep.tile([P, C], U32, name="x_codes%d" % e, align_bytes=64)
-            x_scales[e] = keep.tile([P, C], U8, name="x_scales%d" % e, align_bytes=64)
-            nc.vector.quantize_mx(
-                out=x_codes[e][:].bitcast(FP8X4),
-                scales=x_scales[e][:],
-                in_=grouped[:, C * e : C * (e + 1), :].rearrange("p s j -> p (s j)"),
-            )
-
-        acc_tags = {(3, 1): "h2", (2, 0): "s0", (3, 0): "s1"}
-        y_tags = {0: "s0", 1: "s1", 2: "h2"}
         h_raw, h_codes, h_scales, y_raw, y_ps = {}, {}, {}, {}, {}
 
+        def quant_x(s0, n):
+            codes = keep.tile([P, n], U32, name="x_codes%d" % s0, align_bytes=64)
+            if s0 >= 2 * C:
+                scales = shared.tile([P, n], U8, name="x_scales%d" % s0, align_bytes=64, offset=2 * H + s0 - 2 * C)
+            else:
+                scales = keep.tile([P, n], U8, name="x_scales%d" % s0, align_bytes=64)
+            nc.vector.quantize_mx(
+                out=codes[:].bitcast(FP8X4),
+                scales=scales[:],
+                in_=grouped[:, s0 : s0 + n, :].rearrange("p s j -> p (s j)"),
+            )
+            for b in range(n // 128):
+                x_codes[s0 // 128 + b] = codes[:, 128 * b : 128 * (b + 1)]
+                x_scales[s0 // 128 + b] = scales[:, 128 * b : 128 * (b + 1)]
+
         def layer1(e):
-            h_raw[e] = keep.tile([P, C, 4], BF16, name="h_raw%d" % e, align_bytes=64)
+            if e == 0:
+                h_raw[e] = shared.tile([P, C, 4], BF16, name="h_raw%d" % e, align_bytes=64, offset=0)
+            else:
+                h_raw[e] = keep.tile([P, C, 4], BF16, name="h_raw%d" % e, align_bytes=64, tag="h%d" % e)
             for b in range(2):
-                if (e, b) in acc_tags:
-                    acc = ps_l.tile([P, 4, 128], F32, name="acc_%d%d" % (e, b), tag=acc_tags[e, b])
-                else:
-                    acc = ps_a.tile([P, 4, 128], F32, name="acc")
+                acc = ps_a.tile([P, 4, 128], F32, name="acc")
                 for j in range(4):
-                    w0 = (e * 4 + j) * 128
+                    z0 = (j * E + e) * 128
                     nc.tensor.matmul_mx(
                         out=acc[:, j, :],
-                        lhsT=w1_perm[:, 2 * w0 : 2 * (w0 + 128)].bitcast(FP4X4),
-                        lhsT_scale=s1_perm[:, w0 : w0 + 128],
-                        rhs=x_codes[e][:, 128 * b : 128 * (b + 1)].bitcast(FP8X4),
-                        rhs_scale=x_scales[e][:, 128 * b : 128 * (b + 1)],
+                        lhsT=w1_perm[e][:, 256 * j : 256 * (j + 1)].bitcast(FP4X4),
+                        lhsT_scale=s1_perm[:, z0 : z0 + 128],
+                        rhs=x_codes[2 * e + b].bitcast(FP8X4),
+                        rhs_scale=x_scales[2 * e + b],
                         start=True,
                         stop=True,
                     )
@@ -170,7 +177,7 @@ def tile_moe_two_mlp_gelu_kernel(tc, xT, w1_words, w1_scales, w2_words, w2_scale
                 )
 
         def quant_h(e):
-            h_codes[e] = keep.tile([P, C], U32, name="h_codes%d" % e, align_bytes=64)
+            h_codes[e] = keep.tile([P, C], U32, name="h_codes%d" % e, align_bytes=64, tag="h2" if e == 0 else "h_codes%d" % e)
             h_scales[e] = keep.tile([P, C], U8, name="h_scales%d" % e, align_bytes=64)
             nc.vector.quantize_mx(
                 out=h_codes[e][:].bitcast(FP8X4),
@@ -178,11 +185,8 @@ def tile_moe_two_mlp_gelu_kernel(tc, xT, w1_words, w1_scales, w2_words, w2_scale
                 in_=h_raw[e][:].rearrange("p s j -> p (s j)"),
             )
 
-        def layer2(e, gated=False):
-            if e in y_tags:
-                y_ps[e] = ps_l.tile([P, C], F32, name="y_ps%d" % e, tag=y_tags[e])
-            else:
-                y_ps[e] = ps_y.tile([P, C], F32, name="y_ps")
+        def layer2(e):
+            y_ps[e] = ps_y.tile([P, C], F32, name="y_ps")
             nc.tensor.matmul_mx(
                 out=y_ps[e][:],
                 lhsT=w2_t[:, e, :].bitcast(FP4X4),
@@ -193,15 +197,9 @@ def tile_moe_two_mlp_gelu_kernel(tc, xT, w1_words, w1_scales, w2_words, w2_scale
                 stop=True,
             )
             y_raw[e] = keep.tile([P, C], F32, name="y_raw%d" % e)
-            if gated:
-                nc.vector.tensor_tensor(y_raw[e][:], y_ps[e][:], gate_t[:, C * e : C * (e + 1)], MULT)
-            else:
-                nc.scalar.copy(out=y_raw[e][:], in_=y_ps[e][:])
+            nc.scalar.copy(out=y_raw[e][:], in_=y_ps[e][:])
 
-        def scatter(e, gated=False):
-            if gated:
-                nc.vector.tensor_copy(placed[:].indirect(dst_t[:, 16 * e : 16 * (e + 1)]), y_raw[e][:])
-                return
+        def scatter(e):
             nc.vector.tensor_tensor(
                 placed[:].indirect(dst_t[:, 16 * e : 16 * (e + 1)]),
                 y_raw[e][:],
@@ -209,31 +207,30 @@ def tile_moe_two_mlp_gelu_kernel(tc, xT, w1_words, w1_scales, w2_words, w2_scale
                 MULT,
             )
 
-        gather(0)
-        quant_x(0)
-        permute_words(1, 2)
+        pick(1, 0, 256)
+        permute_words(1)
+        quant_x(0, 256)
         layer1(0)
-        gather(1)
-        quant_x(1)
-        quant_h(0)
-        layer2(0)
+        pick(1, 256, 256)
+        permute_words(2)
+        quant_x(256, 256)
         layer1(1)
-        permute_words(2, 3)
-        gather(2)
-        scatter(0)
-        gather(3)
-        quant_x(2)
-        layer1(2)
-        quant_x(3)
+        pick(1, 512, 512)
+        quant_h(0)
+        quant_x(512, 256)
+        layer2(0)
+        permute_words(3)
+        quant_x(768, 256)
         quant_h(1)
-        permute_words(3, 4)
-        quant_h(2)
+        scatter(0)
+        layer1(2)
         layer2(1)
-        layer1(3)
+        quant_h(2)
         scatter(1)
+        layer1(3)
         layer2(2)
-        scatter(2)
         quant_h(3)
+        scatter(2)
         layer2(3)
         scatter(3)
         nc.sync.dma_start(out=out, in_=placed[:])

@@ -90,10 +90,10 @@ def tile_moe_two_mlp_gelu_kernel(tc, xT, w1_words, w1_scales, w2_words, w2_scale
                 x_raw[h, c] = keep.tile([P, 2, n], F32, name="x_raw%d_%d" % (h, c))
             nc.sync.dma_start(out=x_raw[h, c][:], in_=x_rows[h, :, :, t0 : t0 + n])
 
-        nc.sync.dma_start(offs_t[:], offs)
+        load_scales(s1_raw, w1_scales)
         load_w1(0, 1)
         load_x(0, 0)
-        load_scales(s1_raw, w1_scales)
+        nc.sync.dma_start(offs_t[:], offs)
         for h, c in ((0, 1), (1, 0), (1, 1), (1, 2)):
             load_x(h, c)
         load_w1(1, 2)
@@ -117,10 +117,10 @@ def tile_moe_two_mlp_gelu_kernel(tc, xT, w1_words, w1_scales, w2_words, w2_scale
                 in_=pairs[h][:].rearrange("p t j -> p (t j)").bitcast(U32).indirect(offs_t[:, s0 // 16 : (s0 + n) // 16]),
             )
 
+        permute_scales()
         permute_words(0)
         pair(sc, 0, 0, 0, 512)
         pair(ve, 0, 0, 512, 512)
-        permute_scales()
         pair(sc, 0, 1, 0, 160)
         pair(ve, 0, 1, 160, 352)
         pick(0, 0, 1024)
@@ -233,4 +233,5 @@ def tile_moe_two_mlp_gelu_kernel(tc, xT, w1_words, w1_scales, w2_words, w2_scale
         scatter(2)
         layer2(3)
         scatter(3)
-        nc.sync.dma_start(out=out, in_=placed[:])
+        nc.sync.dma_start(out=out[:, : T // 2], in_=placed[:, : T // 2])
+        nc.scalar.dma_start(out=out[:, T // 2 :], in_=placed[:, T // 2 :])

@@ -61,10 +61,7 @@ def tile_moe_two_mlp_gelu_kernel(tc, xT, w1_words, w1_scales, w2_words, w2_scale
                 )
 
         def permute_words(e):
-            if e == 3:
-                w1_perm[e] = shared.tile([P, 2 * H], U8, name="w1_perm%d" % e, align_bytes=64, offset=0)
-            else:
-                w1_perm[e] = keep.tile([P, 2 * H], U8, name="w1_perm%d" % e, align_bytes=64)
+            w1_perm[e] = keep.tile([P, 2 * H], U8, name="w1_perm%d" % e, align_bytes=64)
             nc.vector.tensor_copy(
                 out=w1_perm[e][:].bitcast(U16).rearrange("p (j c) -> p j c", j=4),
                 in_=w1_raw[e].bitcast(U16).rearrange("p (c j) -> p j c", j=4),
@@ -91,14 +88,14 @@ def tile_moe_two_mlp_gelu_kernel(tc, xT, w1_words, w1_scales, w2_words, w2_scale
             nc.sync.dma_start(out=x_raw[h, c][:], in_=x_rows[h, :, :, t0 : t0 + n])
 
         load_scales(s1_raw, w1_scales)
-        load_w1(0, 1)
         load_x(0, 0)
         nc.sync.dma_start(offs_t[:], offs)
         for h, c in ((0, 1), (1, 0), (1, 1), (1, 2)):
             load_x(h, c)
+        load_w1(0, 1)
         load_w1(1, 2)
-        load_w1(2, 4)
         load_scales(s2_t, w2_scales)
+        load_w1(2, 4)
         nc.sync.dma_start(dst_t[:], dst)
 
         def pair(engine_copy, h, c, a, n):
@@ -118,7 +115,6 @@ def tile_moe_two_mlp_gelu_kernel(tc, xT, w1_words, w1_scales, w2_words, w2_scale
             )
 
         permute_scales()
-        permute_words(0)
         pair(sc, 0, 0, 0, 512)
         pair(ve, 0, 0, 512, 512)
         pair(sc, 0, 1, 0, 160)
@@ -135,7 +131,8 @@ def tile_moe_two_mlp_gelu_kernel(tc, xT, w1_words, w1_scales, w2_words, w2_scale
         nc.scalar.dma_start(out=gate_t[:], in_=gate)
 
         x_codes, x_scales = {}, {}
-        h_raw, h_codes, h_scales, y_raw, y_ps = {}, {}, {}, {}, {}
+        h_raw, h_codes, h_scales, y_raw = {}, {}, {}, {}
+        pieces = [[(0, 128), (128, 256)]] + [[(0, 256)]] * (E - 1)
 
         def quant_x(s0, n):
             codes = keep.tile([P, n], U32, name="x_codes%d" % s0, align_bytes=64)
@@ -179,25 +176,27 @@ def tile_moe_two_mlp_gelu_kernel(tc, xT, w1_words, w1_scales, w2_words, w2_scale
         def quant_h(e):
             h_codes[e] = keep.tile([P, C], U32, name="h_codes%d" % e, align_bytes=64, tag="h2" if e == 0 else "h_codes%d" % e)
             h_scales[e] = keep.tile([P, C], U8, name="h_scales%d" % e, align_bytes=64)
-            nc.vector.quantize_mx(
-                out=h_codes[e][:].bitcast(FP8X4),
-                scales=h_scales[e][:],
-                in_=h_raw[e][:].rearrange("p s j -> p (s j)"),
-            )
+            for s0, s1 in pieces[e]:
+                nc.vector.quantize_mx(
+                    out=h_codes[e][:, s0:s1].bitcast(FP8X4),
+                    scales=h_scales[e][:, s0:s1],
+                    in_=h_raw[e][:, s0:s1, :].rearrange("p s j -> p (s j)"),
+                )
 
         def layer2(e):
-            y_ps[e] = ps_y.tile([P, C], F32, name="y_ps")
-            nc.tensor.matmul_mx(
-                out=y_ps[e][:],
-                lhsT=w2_t[:, e, :].bitcast(FP4X4),
-                lhsT_scale=s2_t[:, e, :],
-                rhs=h_codes[e][:].bitcast(FP8X4),
-                rhs_scale=h_scales[e][:],
-                start=True,
-                stop=True,
-            )
             y_raw[e] = keep.tile([P, C], F32, name="y_raw%d" % e)
-            nc.scalar.copy(out=y_raw[e][:], in_=y_ps[e][:])
+            for s0, s1 in pieces[e]:
+                y_ps = ps_y.tile([P, s1 - s0], F32, name="y_ps")
+                nc.tensor.matmul_mx(
+                    out=y_ps[:],
+                    lhsT=w2_t[:, e, :].bitcast(FP4X4),
+                    lhsT_scale=s2_t[:, e, :],
+                    rhs=h_codes[e][:, s0:s1].bitcast(FP8X4),
+                    rhs_scale=h_scales[e][:, s0:s1],
+                    start=True,
+                    stop=True,
+                )
+                nc.scalar.copy(out=y_raw[e][:, s0:s1], in_=y_ps[:])
 
         def scatter(e):
             nc.vector.tensor_tensor(
@@ -208,17 +207,21 @@ def tile_moe_two_mlp_gelu_kernel(tc, xT, w1_words, w1_scales, w2_words, w2_scale
             )
 
         pick(1, 0, 256)
-        permute_words(1)
-        quant_x(0, 256)
+        permute_words(0)
+        quant_x(0, 128)
+        quant_x(128, 128)
         layer1(0)
         pick(1, 256, 256)
-        permute_words(2)
-        quant_x(256, 256)
+        permute_words(1)
+        quant_x(256, 128)
+        quant_x(384, 128)
         layer1(1)
         pick(1, 512, 512)
         quant_h(0)
-        quant_x(512, 256)
         layer2(0)
+        permute_words(2)
+        quant_x(512, 128)
+        quant_x(640, 128)
         permute_words(3)
         quant_x(768, 256)
         quant_h(1)

@@ -76,12 +76,12 @@ def tile_moe_two_mlp_gelu_kernel(tc, xT, w1_words, w1_scales, w2_words, w2_scale
         pairs = [keep.tile([P, T, 2], BF16, name="pairs%d" % h, align_bytes=64) for h in range(2)]
         grouped = keep.tile([P, S, 4], BF16, name="grouped", align_bytes=64)
         x_rows = xT.rearrange("(p h j) t -> h p j t", h=2, j=2)
-        chunks = [[(0, 1024), (1024, 512)], [(0, 512), (512, 512), (1024, 512)]]
+        chunks = [[(0, 768), (768, 512), (1280, 256)], [(0, 512), (512, 512), (1024, 320), (1344, 192)]]
         x_raw = {}
 
         def load_x(h, c):
             t0, n = chunks[h][c]
-            if (h, c) == (1, 2):
+            if (h, c) == (1, 3):
                 x_raw[h, c] = late.tile([P, 2, n], F32, name="x_raw%d_%d" % (h, c), align_bytes=64, offset=0)
             else:
                 x_raw[h, c] = keep.tile([P, 2, n], F32, name="x_raw%d_%d" % (h, c))
@@ -90,7 +90,7 @@ def tile_moe_two_mlp_gelu_kernel(tc, xT, w1_words, w1_scales, w2_words, w2_scale
         load_scales(s1_raw, w1_scales)
         load_x(0, 0)
         nc.sync.dma_start(offs_t[:], offs)
-        for h, c in ((0, 1), (1, 0), (1, 1), (1, 2)):
+        for h, c in ((0, 1), (0, 2), (1, 0), (1, 1), (1, 2), (1, 3)):
             load_x(h, c)
         load_w1(0, 1)
         load_w1(1, 2)
@@ -115,16 +115,18 @@ def tile_moe_two_mlp_gelu_kernel(tc, xT, w1_words, w1_scales, w2_words, w2_scale
             )
 
         permute_scales()
-        pair(sc, 0, 0, 0, 512)
-        pair(ve, 0, 0, 512, 512)
-        pair(sc, 0, 1, 0, 160)
-        pair(ve, 0, 1, 160, 352)
+        pair(sc, 0, 0, 0, 384)
+        pair(ve, 0, 0, 384, 384)
+        pair(sc, 0, 1, 0, 192)
+        pair(ve, 0, 1, 192, 320)
+        pair(sc, 0, 2, 0, 64)
+        pair(ve, 0, 2, 64, 192)
         pick(0, 0, 1024)
         pair(sc, 1, 0, 0, 512)
-        pair(sc, 1, 1, 0, 256)
-        pair(ve, 1, 1, 256, 256)
-        pair(sc, 1, 2, 0, 160)
-        pair(ve, 1, 2, 160, 352)
+        pair(sc, 1, 1, 0, 512)
+        pair(ve, 1, 2, 0, 320)
+        pair(sc, 1, 3, 0, 48)
+        pair(ve, 1, 3, 48, 144)
         w2_t = late.tile([P, E, 2 * N], U8, name="w2_t", align_bytes=64, offset=0)
         gate_t = late.tile([P, S], F32, name="gate_t", align_bytes=64, offset=E * 2 * N)
         nc.scalar.dma_start(out=w2_t[:].bitcast(I32), in_=w2_words[:, 0].rearrange("e p b -> p e b").bitcast(I32))

@@ -74,7 +74,8 @@ def tile_moe_two_mlp_gelu_kernel(tc, xT, w1_words, w1_scales, w2_words, w2_scale
             )
 
         pairs = [keep.tile([P, T, 2], BF16, name="pairs%d" % h, align_bytes=64) for h in range(2)]
-        grouped = keep.tile([P, S, 4], BF16, name="grouped", align_bytes=64)
+        grouped = {0: keep.tile([P, S // 2, 4], BF16, name="grouped0", align_bytes=64)}
+        first_pairs = keep.tile([P, S // 2], U32, name="first_pairs", align_bytes=64)
         x_rows = xT.rearrange("(p h j) t -> h p j t", h=2, j=2)
         chunks = [[(0, 768), (768, 512), (1280, 256)], [(0, 512), (512, 512), (1024, 320), (1344, 192)]]
         x_raw = {}
@@ -82,7 +83,7 @@ def tile_moe_two_mlp_gelu_kernel(tc, xT, w1_words, w1_scales, w2_words, w2_scale
         def load_x(h, c):
             t0, n = chunks[h][c]
             if (h, c) == (1, 3):
-                x_raw[h, c] = late.tile([P, 2, n], F32, name="x_raw%d_%d" % (h, c), align_bytes=64, offset=0)
+                x_raw[h, c] = late.tile([P, 2, n], F32, name="x_raw%d_%d" % (h, c), align_bytes=64, offset=3840)
             else:
                 x_raw[h, c] = keep.tile([P, 2, n], F32, name="x_raw%d_%d" % (h, c))
             nc.sync.dma_start(out=x_raw[h, c][:], in_=x_rows[h, :, :, t0 : t0 + n])
@@ -106,13 +107,19 @@ def tile_moe_two_mlp_gelu_kernel(tc, xT, w1_words, w1_scales, w2_words, w2_scale
             )
 
         sc, ve = nc.scalar.copy, nc.vector.tensor_copy
-        slot_words = grouped[:].rearrange("p s j -> p (s j)").bitcast(U32).rearrange("p (s h) -> p s h", h=2)
 
-        def pick(h, s0, n):
+        def slot_words(s0, n, h):
+            words = grouped[s0 // 512][:].rearrange("p s j -> p (s j)").bitcast(U32).rearrange("p (s h) -> p s h", h=2)
+            return words[:, s0 % 512 : s0 % 512 + n, h]
+
+        def gather(out_words, h, s0, n):
             nc.vector.tensor_copy(
-                out=slot_words[:, s0 : s0 + n, h],
+                out=out_words,
                 in_=pairs[h][:].rearrange("p t j -> p (t j)").bitcast(U32).indirect(offs_t[:, s0 // 16 : (s0 + n) // 16]),
             )
+
+        def pick(h, s0, n):
+            gather(slot_words(s0, n, h), h, s0, n)
 
         permute_scales()
         pair(sc, 0, 0, 0, 384)
@@ -121,16 +128,19 @@ def tile_moe_two_mlp_gelu_kernel(tc, xT, w1_words, w1_scales, w2_words, w2_scale
         pair(ve, 0, 1, 192, 320)
         pair(sc, 0, 2, 0, 64)
         pair(ve, 0, 2, 64, 192)
-        pick(0, 0, 1024)
+        pick(0, 0, 512)
+        gather(first_pairs[:], 0, 512, 512)
         pair(sc, 1, 0, 0, 512)
         pair(sc, 1, 1, 0, 512)
         pair(ve, 1, 2, 0, 320)
         pair(sc, 1, 3, 0, 48)
         pair(ve, 1, 3, 48, 144)
-        w2_t = late.tile([P, E, 2 * N], U8, name="w2_t", align_bytes=64, offset=0)
-        gate_t = late.tile([P, S], F32, name="gate_t", align_bytes=64, offset=E * 2 * N)
+        w2_t = late.tile([P, E, 2 * N], U8, name="w2_t", align_bytes=64, offset=4096)
+        gate_t = late.tile([P, S], F32, name="gate_t", align_bytes=64, offset=0)
+        grouped[1] = late.tile([P, S // 2, 4], BF16, name="grouped1", align_bytes=64, offset=5120)
         nc.scalar.dma_start(out=w2_t[:].bitcast(I32), in_=w2_words[:, 0].rearrange("e p b -> p e b").bitcast(I32))
         nc.scalar.dma_start(out=gate_t[:], in_=gate)
+        nc.scalar.copy(out=slot_words(512, 512, 0), in_=first_pairs[:])
 
         x_codes, x_scales = {}, {}
         h_raw, h_codes, h_scales, y_raw = {}, {}, {}, {}
@@ -145,7 +155,7 @@ def tile_moe_two_mlp_gelu_kernel(tc, xT, w1_words, w1_scales, w2_words, w2_scale
             nc.vector.quantize_mx(
                 out=codes[:].bitcast(FP8X4),
                 scales=scales[:],
-                in_=grouped[:, s0 : s0 + n, :].rearrange("p s j -> p (s j)"),
+                in_=grouped[s0 // 512][:, s0 % 512 : s0 % 512 + n, :].rearrange("p s j -> p (s j)"),
             )
             for b in range(n // 128):
                 x_codes[s0 // 128 + b] = codes[:, 128 * b : 128 * (b + 1)]

@@ -74,8 +74,8 @@ def tile_moe_two_mlp_gelu_kernel(tc, xT, w1_words, w1_scales, w2_words, w2_scale
             )
 
         pairs = [keep.tile([P, T, 2], BF16, name="pairs%d" % h, align_bytes=64) for h in range(2)]
-        grouped = {0: keep.tile([P, S // 2, 4], BF16, name="grouped0", align_bytes=64)}
-        first_pairs = keep.tile([P, S // 2], U32, name="first_pairs", align_bytes=64)
+        grouped = keep.tile([P, S, 4], BF16, name="grouped", align_bytes=64)
+        picked = keep.tile([P, 3, S // 2], U32, name="picked", align_bytes=64)
         x_rows = xT.rearrange("(p h j) t -> h p j t", h=2, j=2)
         chunks = [[(0, 768), (768, 512), (1280, 256)], [(0, 512), (512, 512), (1024, 320), (1344, 192)]]
         x_raw = {}
@@ -83,7 +83,7 @@ def tile_moe_two_mlp_gelu_kernel(tc, xT, w1_words, w1_scales, w2_words, w2_scale
         def load_x(h, c):
             t0, n = chunks[h][c]
             if (h, c) == (1, 3):
-                x_raw[h, c] = late.tile([P, 2, n], F32, name="x_raw%d_%d" % (h, c), align_bytes=64, offset=3840)
+                x_raw[h, c] = late.tile([P, 2, n], F32, name="x_raw%d_%d" % (h, c), align_bytes=64, offset=0)
             else:
                 x_raw[h, c] = keep.tile([P, 2, n], F32, name="x_raw%d_%d" % (h, c))
             nc.sync.dma_start(out=x_raw[h, c][:], in_=x_rows[h, :, :, t0 : t0 + n])
@@ -107,10 +107,7 @@ def tile_moe_two_mlp_gelu_kernel(tc, xT, w1_words, w1_scales, w2_words, w2_scale
             )
 
         sc, ve = nc.scalar.copy, nc.vector.tensor_copy
-
-        def slot_words(s0, n, h):
-            words = grouped[s0 // 512][:].rearrange("p s j -> p (s j)").bitcast(U32).rearrange("p (s h) -> p s h", h=2)
-            return words[:, s0 % 512 : s0 % 512 + n, h]
+        slot_words = grouped[:].rearrange("p s j -> p (s j)").bitcast(U32).rearrange("p (s h) -> p s h", h=2)
 
         def gather(out_words, h, s0, n):
             nc.vector.tensor_copy(
@@ -118,8 +115,22 @@ def tile_moe_two_mlp_gelu_kernel(tc, xT, w1_words, w1_scales, w2_words, w2_scale
                 in_=pairs[h][:].rearrange("p t j -> p (t j)").bitcast(U32).indirect(offs_t[:, s0 // 16 : (s0 + n) // 16]),
             )
 
-        def pick(h, s0, n):
-            gather(slot_words(s0, n, h), h, s0, n)
+        def pick(s0, n):
+            gather(picked[:, 2, s0 % 512 : s0 % 512 + n], 1, s0, n)
+
+        views = {
+            U32: (picked[:], slot_words),
+            I32: (
+                picked[:].bitcast(I32),
+                grouped[:].rearrange("p s j -> p (s j)").bitcast(I32).rearrange("p (s h) -> p s h", h=2),
+            ),
+        }
+
+        def weave(engine_copy, dtype, s0, n):
+            row = s0 // 512
+            source, target = views[dtype]
+            both = source[:, row : 3 : 2 - row, s0 % 512 : s0 % 512 + n]
+            engine_copy(out=target[:, s0 : s0 + n, :], in_=both.rearrange("p h s -> p s h"))
 
         permute_scales()
         pair(sc, 0, 0, 0, 384)
@@ -128,19 +139,16 @@ def tile_moe_two_mlp_gelu_kernel(tc, xT, w1_words, w1_scales, w2_words, w2_scale
         pair(ve, 0, 1, 192, 320)
         pair(sc, 0, 2, 0, 64)
         pair(ve, 0, 2, 64, 192)
-        pick(0, 0, 512)
-        gather(first_pairs[:], 0, 512, 512)
+        gather(picked[:, 0:2, :].rearrange("p r s -> p (r s)"), 0, 0, S)
         pair(sc, 1, 0, 0, 512)
         pair(sc, 1, 1, 0, 512)
         pair(ve, 1, 2, 0, 320)
         pair(sc, 1, 3, 0, 48)
         pair(ve, 1, 3, 48, 144)
-        w2_t = late.tile([P, E, 2 * N], U8, name="w2_t", align_bytes=64, offset=4096)
-        gate_t = late.tile([P, S], F32, name="gate_t", align_bytes=64, offset=0)
-        grouped[1] = late.tile([P, S // 2, 4], BF16, name="grouped1", align_bytes=64, offset=5120)
+        w2_t = late.tile([P, E, 2 * N], U8, name="w2_t", align_bytes=64, offset=0)
+        gate_t = late.tile([P, S], F32, name="gate_t", align_bytes=64, offset=E * 2 * N)
         nc.scalar.dma_start(out=w2_t[:].bitcast(I32), in_=w2_words[:, 0].rearrange("e p b -> p e b").bitcast(I32))
         nc.scalar.dma_start(out=gate_t[:], in_=gate)
-        nc.scalar.copy(out=slot_words(512, 512, 0), in_=first_pairs[:])
 
         x_codes, x_scales = {}, {}
         h_raw, h_codes, h_scales, y_raw = {}, {}, {}, {}
@@ -155,7 +163,7 @@ def tile_moe_two_mlp_gelu_kernel(tc, xT, w1_words, w1_scales, w2_words, w2_scale
             nc.vector.quantize_mx(
                 out=codes[:].bitcast(FP8X4),
                 scales=scales[:],
-                in_=grouped[s0 // 512][:, s0 % 512 : s0 % 512 + n, :].rearrange("p s j -> p (s j)"),
+                in_=grouped[:, s0 : s0 + n, :].rearrange("p s j -> p (s j)"),
             )
             for b in range(n // 128):
                 x_codes[s0 // 128 + b] = codes[:, 128 * b : 128 * (b + 1)]
@@ -218,17 +226,21 @@ def tile_moe_two_mlp_gelu_kernel(tc, xT, w1_words, w1_scales, w2_words, w2_scale
                 MULT,
             )
 
-        pick(1, 0, 256)
+        pick(0, 256)
+        weave(sc, U32, 0, 128)
+        weave(sc, U32, 128, 128)
+        pick(256, 256)
+        weave(sc, U32, 256, 256)
         permute_words(0)
         quant_x(0, 128)
         quant_x(128, 128)
         layer1(0)
-        pick(1, 256, 256)
         permute_words(1)
         quant_x(256, 128)
         quant_x(384, 128)
         layer1(1)
-        pick(1, 512, 512)
+        pick(512, 512)
+        weave(ve, I32, 512, 512)
         quant_h(0)
         layer2(0)
         permute_words(2)

@@ -30,15 +30,17 @@ def tile_moe_two_mlp_gelu_kernel(tc, xT, w1_words, w1_scales, w2_words, w2_scale
 
         offs_t = keep.tile([P, S // 16], U16, name="offs_t")
         dst_t = keep.tile([P, S // 16], U16, name="dst_t")
-        s1_raw = keep.tile([P, E, H], U8, name="s1_raw", align_bytes=64)
-        s1_perm = keep.tile([P, E * H], U8, name="s1_perm", align_bytes=64)
+        s1_raw = keep.tile([P, H], U8, name="s1_raw", align_bytes=64)
+        s1_perm = keep.tile([P, H], U8, name="s1_perm", align_bytes=64)
+        s1_low = keep.tile([P, E - 1, H], U8, name="s1_low", align_bytes=64)
         s2_t = keep.tile([P, E, N], U8, name="s2_t", align_bytes=64)
         placed = keep.tile([P, T], F32, name="placed")
         warm = keep.tile([P, 1], F32, name="warm")
 
-        nc.gpsimd.memset(s1_raw[:].rearrange("p e i -> p (e i)").bitcast(I32), 0)
+        nc.gpsimd.memset(s1_raw[:].bitcast(I32), 0)
         nc.vector.memset(warm[:], 0.0)
         nc.scalar.activation(out=warm[:], in_=warm[:], func=GELU)
+        nc.gpsimd.memset(s1_low[:].rearrange("p e i -> p (e i)").bitcast(I32), 0)
         nc.gpsimd.memset(s2_t[:].rearrange("p e i -> p (e i)").bitcast(I32), 0)
         nc.gpsimd.memset(placed[:], 0.0)
 
@@ -60,6 +62,19 @@ def tile_moe_two_mlp_gelu_kernel(tc, xT, w1_words, w1_scales, w2_words, w2_scale
                     in_=scales[:, 0, 4 * q : 4 * q + 4, :].rearrange("e q i -> q e i").bitcast(I32),
                 )
 
+        def load_packed_scales():
+            for q in range(4):
+                nc.sync.dma_start(
+                    out=s1_raw[32 * q : 32 * q + 4 * E, :].bitcast(I32),
+                    in_=w1_scales[:, 0, 4 * q : 4 * q + 4, :].bitcast(I32),
+                )
+
+        def lower_scales(e):
+            nc.sync.dma_start(
+                out=s1_low[0:100, e - 1, :].bitcast(I32),
+                in_=s1_perm[4 * e : 4 * e + 100, :].bitcast(I32),
+            )
+
         def permute_words(e):
             w1_perm[e] = keep.tile([P, 2 * H], U8, name="w1_perm%d" % e, align_bytes=64)
             nc.vector.tensor_copy(
@@ -70,7 +85,7 @@ def tile_moe_two_mlp_gelu_kernel(tc, xT, w1_words, w1_scales, w2_words, w2_scale
         def permute_scales():
             nc.vector.tensor_copy(
                 out=s1_perm[:].rearrange("p (j c) -> p j c", j=4),
-                in_=s1_raw[:].rearrange("p e (m j) -> p j (e m)", j=4),
+                in_=s1_raw[:].rearrange("p (m j) -> p j m", j=4),
             )
 
         pairs = [keep.tile([P, T, 2], BF16, name="pairs%d" % h, align_bytes=64) for h in range(2)]
@@ -88,16 +103,19 @@ def tile_moe_two_mlp_gelu_kernel(tc, xT, w1_words, w1_scales, w2_words, w2_scale
                 x_raw[h, c] = keep.tile([P, 2, n], F32, name="x_raw%d_%d" % (h, c))
             nc.sync.dma_start(out=x_raw[h, c][:], in_=x_rows[h, :, :, t0 : t0 + n])
 
-        load_scales(s1_raw, w1_scales)
         load_x(0, 0)
         nc.sync.dma_start(offs_t[:], offs)
+        load_packed_scales()
         for h, c in ((0, 1), (0, 2), (1, 0), (1, 1), (1, 2), (1, 3)):
             load_x(h, c)
-        load_w1(0, 1)
-        load_w1(1, 2)
+        permute_scales()
+        load_w1(0, 2)
+        lower_scales(1)
         load_scales(s2_t, w2_scales)
         load_w1(2, 4)
         nc.sync.dma_start(dst_t[:], dst)
+        lower_scales(2)
+        lower_scales(3)
 
         def pair(engine_copy, h, c, a, n):
             t0 = chunks[h][c][0]
@@ -132,7 +150,6 @@ def tile_moe_two_mlp_gelu_kernel(tc, xT, w1_words, w1_scales, w2_words, w2_scale
             both = source[:, row : 3 : 2 - row, s0 % 512 : s0 % 512 + n]
             engine_copy(out=target[:, s0 : s0 + n, :], in_=both.rearrange("p h s -> p s h"))
 
-        permute_scales()
         pair(sc, 0, 0, 0, 384)
         pair(ve, 0, 0, 384, 384)
         pair(sc, 0, 1, 0, 192)
@@ -177,11 +194,10 @@ def tile_moe_two_mlp_gelu_kernel(tc, xT, w1_words, w1_scales, w2_words, w2_scale
             for b in range(2):
                 acc = ps_a.tile([P, 4, 128], F32, name="acc")
                 for j in range(4):
-                    z0 = (j * E + e) * 128
                     nc.tensor.matmul_mx(
                         out=acc[:, j, :],
                         lhsT=w1_perm[e][:, 256 * j : 256 * (j + 1)].bitcast(FP4X4),
-                        lhsT_scale=s1_perm[:, z0 : z0 + 128],
+                        lhsT_scale=(s1_perm[:] if e == 0 else s1_low[:, e - 1, :])[:, 128 * j : 128 * (j + 1)],
                         rhs=x_codes[2 * e + b].bitcast(FP8X4),
                         rhs_scale=x_scales[2 * e + b],
                         start=True,

@@ -92,22 +92,23 @@ def tile_moe_two_mlp_gelu_kernel(tc, xT, w1_words, w1_scales, w2_words, w2_scale
         grouped = keep.tile([P, S, 4], BF16, name="grouped", align_bytes=64)
         picked = keep.tile([P, 3, S // 2], U32, name="picked", align_bytes=64)
         x_rows = xT.rearrange("(p h j) t -> h p j t", h=2, j=2)
-        chunks = [[(0, 768), (768, 512), (1280, 256)], [(0, 512), (512, 512), (1024, 320), (1344, 192)]]
+        chunks = [[(0, 1152), (1152, 384)], [(0, 768), (768, 576), (1344, 192)]]
         x_raw = {}
 
         def load_x(h, c):
             t0, n = chunks[h][c]
-            if (h, c) == (1, 3):
+            if (h, c) == (1, 2):
                 x_raw[h, c] = late.tile([P, 2, n], F32, name="x_raw%d_%d" % (h, c), align_bytes=64, offset=0)
             else:
                 x_raw[h, c] = keep.tile([P, 2, n], F32, name="x_raw%d_%d" % (h, c))
             nc.sync.dma_start(out=x_raw[h, c][:], in_=x_rows[h, :, :, t0 : t0 + n])
 
         load_x(0, 0)
-        nc.sync.dma_start(offs_t[:], offs)
         load_packed_scales()
-        for h, c in ((0, 1), (0, 2), (1, 0), (1, 1), (1, 2), (1, 3)):
-            load_x(h, c)
+        load_x(0, 1)
+        nc.sync.dma_start(offs_t[:], offs)
+        for c in range(3):
+            load_x(1, c)
         permute_scales()
         load_w1(0, 2)
         lower_scales(1)
@@ -120,8 +121,8 @@ def tile_moe_two_mlp_gelu_kernel(tc, xT, w1_words, w1_scales, w2_words, w2_scale
         def pair(engine_copy, h, c, a, n):
             t0 = chunks[h][c][0]
             engine_copy(
-                out=pairs[h][:, t0 + a : t0 + a + n, :].rearrange("p (c i) j -> p c j i", i=4),
-                in_=x_raw[h, c][:, :, a : a + n].rearrange("p j (c i) -> p c j i", i=4),
+                out=pairs[h][:, t0 + a : t0 + a + n, :],
+                in_=x_raw[h, c][:, :, a : a + n].rearrange("p j t -> p t j"),
             )
 
         sc, ve = nc.scalar.copy, nc.vector.tensor_copy
@@ -150,18 +151,17 @@ def tile_moe_two_mlp_gelu_kernel(tc, xT, w1_words, w1_scales, w2_words, w2_scale
             both = source[:, row : 3 : 2 - row, s0 % 512 : s0 % 512 + n]
             engine_copy(out=target[:, s0 : s0 + n, :], in_=both.rearrange("p h s -> p s h"))
 
-        pair(sc, 0, 0, 0, 384)
-        pair(ve, 0, 0, 384, 384)
-        pair(sc, 0, 1, 0, 192)
-        pair(ve, 0, 1, 192, 320)
-        pair(sc, 0, 2, 0, 64)
-        pair(ve, 0, 2, 64, 192)
+        pair(sc, 0, 0, 0, 448)
+        pair(ve, 0, 0, 448, 704)
+        pair(sc, 0, 1, 0, 112)
+        pair(ve, 0, 1, 112, 272)
         gather(picked[:, 0:2, :].rearrange("p r s -> p (r s)"), 0, 0, S)
-        pair(sc, 1, 0, 0, 512)
-        pair(sc, 1, 1, 0, 512)
-        pair(ve, 1, 2, 0, 320)
-        pair(sc, 1, 3, 0, 48)
-        pair(ve, 1, 3, 48, 144)
+        pair(sc, 1, 0, 0, 576)
+        pair(ve, 1, 0, 576, 192)
+        pair(sc, 1, 1, 0, 224)
+        pair(ve, 1, 1, 224, 352)
+        pair(sc, 1, 2, 0, 48)
+        pair(ve, 1, 2, 48, 144)
         w2_t = late.tile([P, E, 2 * N], U8, name="w2_t", align_bytes=64, offset=0)
         gate_t = late.tile([P, S], F32, name="gate_t", align_bytes=64, offset=E * 2 * N)
         nc.scalar.dma_start(out=w2_t[:].bitcast(I32), in_=w2_words[:, 0].rearrange("e p b -> p e b").bitcast(I32))

@@ -30,18 +30,16 @@ def tile_moe_two_mlp_gelu_kernel(tc, xT, w1_words, w1_scales, w2_words, w2_scale
 
         offs_t = keep.tile([P, S // 16], U16, name="offs_t")
         dst_t = keep.tile([P, S // 16], U16, name="dst_t")
-        s1_raw = keep.tile([P, H], U8, name="s1_raw", align_bytes=64)
-        s1_perm = keep.tile([P, H], U8, name="s1_perm", align_bytes=64)
-        s1_low = keep.tile([P, E - 1, H], U8, name="s1_low", align_bytes=64)
-        s2_t = keep.tile([P, E, N], U8, name="s2_t", align_bytes=64)
+        s1_raw = keep.tile([P, E * H], U8, name="s1_raw", align_bytes=64)
+        s1_perm = keep.tile([P, E * (H + N)], U8, name="s1_perm", align_bytes=64)
+        s2_t = s1_perm[:, E * H :].rearrange("p (e i) -> p e i", e=E)
         placed = keep.tile([P, T], F32, name="placed")
         warm = keep.tile([P, 1], F32, name="warm")
 
         nc.gpsimd.memset(s1_raw[:].bitcast(I32), 0)
         nc.vector.memset(warm[:], 0.0)
         nc.scalar.activation(out=warm[:], in_=warm[:], func=GELU)
-        nc.gpsimd.memset(s1_low[:].rearrange("p e i -> p (e i)").bitcast(I32), 0)
-        nc.gpsimd.memset(s2_t[:].rearrange("p e i -> p (e i)").bitcast(I32), 0)
+        nc.gpsimd.memset(s1_perm[:, E * H :].bitcast(I32), 0)
         nc.gpsimd.memset(placed[:], 0.0)
 
         w1_raw, w1_perm = {}, {}
@@ -55,24 +53,22 @@ def tile_moe_two_mlp_gelu_kernel(tc, xT, w1_words, w1_scales, w2_words, w2_scale
             for e in range(e0, e1):
                 w1_raw[e] = raw[:, 2 * H * (e - e0) : 2 * H * (e - e0 + 1)]
 
-        def load_scales(tile, scales):
-            for q in range(4):
-                nc.sync.dma_start(
-                    out=tile[32 * q : 32 * q + 4, :, :].bitcast(I32),
-                    in_=scales[:, 0, 4 * q : 4 * q + 4, :].rearrange("e q i -> q e i").bitcast(I32),
-                )
-
         def load_packed_scales():
-            for q in range(4):
-                nc.sync.dma_start(
-                    out=s1_raw[32 * q : 32 * q + 4 * E, :].bitcast(I32),
-                    in_=w1_scales[:, 0, 4 * q : 4 * q + 4, :].bitcast(I32),
-                )
-
-        def lower_scales(e):
             nc.sync.dma_start(
-                out=s1_low[0:100, e - 1, :].bitcast(I32),
-                in_=s1_perm[4 * e : 4 * e + 100, :].bitcast(I32),
+                out=s1_raw[0:P:8, :].rearrange("q (e i) -> q e i", e=E).bitcast(I32),
+                in_=w1_scales[:, 0].rearrange("e q i -> q e i").bitcast(I32),
+            )
+
+        def load_second_scales():
+            nc.sync.dma_start(
+                out=s1_perm[0:P:8, E * H :].rearrange("q (e i) -> q e i", e=E).bitcast(I32),
+                in_=w2_scales[:, 0].rearrange("e q i -> q e i").bitcast(I32),
+            )
+
+        def lower_scales(r):
+            nc.sync.dma_start(
+                out=s1_perm[r:P:32, :].bitcast(I32),
+                in_=s1_perm[8 * r : P : 32, :].bitcast(I32),
             )
 
         def permute_words(e):
@@ -84,15 +80,15 @@ def tile_moe_two_mlp_gelu_kernel(tc, xT, w1_words, w1_scales, w2_words, w2_scale
 
         def permute_scales():
             nc.vector.tensor_copy(
-                out=s1_perm[:].rearrange("p (j c) -> p j c", j=4),
-                in_=s1_raw[:].rearrange("p (m j) -> p j m", j=4),
+                out=s1_perm[:, : E * H].rearrange("p (e j c) -> p e j c", e=E, j=4),
+                in_=s1_raw[:].rearrange("p (e m j) -> p e j m", e=E, j=4),
             )
 
         pairs = [keep.tile([P, T, 2], BF16, name="pairs%d" % h, align_bytes=64) for h in range(2)]
         grouped = keep.tile([P, S, 4], BF16, name="grouped", align_bytes=64)
         picked = keep.tile([P, 3, S // 2], U32, name="picked", align_bytes=64)
         x_rows = xT.rearrange("(p h j) t -> h p j t", h=2, j=2)
-        chunks = [[(0, 1152), (1152, 384)], [(0, 768), (768, 576), (1344, 192)]]
+        chunks = [[(0, 896), (896, 640)], [(0, 768), (768, 576), (1344, 192)]]
         x_raw = {}
 
         def load_x(h, c):
@@ -107,16 +103,15 @@ def tile_moe_two_mlp_gelu_kernel(tc, xT, w1_words, w1_scales, w2_words, w2_scale
         load_packed_scales()
         load_x(0, 1)
         nc.sync.dma_start(offs_t[:], offs)
+        load_second_scales()
         for c in range(3):
             load_x(1, c)
         permute_scales()
         load_w1(0, 2)
-        lower_scales(1)
-        load_scales(s2_t, w2_scales)
+        for r in range(1, 4):
+            lower_scales(r)
         load_w1(2, 4)
         nc.sync.dma_start(dst_t[:], dst)
-        lower_scales(2)
-        lower_scales(3)
 
         def pair(engine_copy, h, c, a, n):
             t0 = chunks[h][c][0]
@@ -151,10 +146,10 @@ def tile_moe_two_mlp_gelu_kernel(tc, xT, w1_words, w1_scales, w2_words, w2_scale
             both = source[:, row : 3 : 2 - row, s0 % 512 : s0 % 512 + n]
             engine_copy(out=target[:, s0 : s0 + n, :], in_=both.rearrange("p h s -> p s h"))
 
-        pair(sc, 0, 0, 0, 448)
-        pair(ve, 0, 0, 448, 704)
-        pair(sc, 0, 1, 0, 112)
-        pair(ve, 0, 1, 112, 272)
+        pair(sc, 0, 0, 0, 608)
+        pair(ve, 0, 0, 608, 288)
+        pair(sc, 0, 1, 0, 208)
+        pair(ve, 0, 1, 208, 432)
         gather(picked[:, 0:2, :].rearrange("p r s -> p (r s)"), 0, 0, S)
         pair(sc, 1, 0, 0, 576)
         pair(ve, 1, 0, 576, 192)
@@ -197,7 +192,7 @@ def tile_moe_two_mlp_gelu_kernel(tc, xT, w1_words, w1_scales, w2_words, w2_scale
                     nc.tensor.matmul_mx(
                         out=acc[:, j, :],
                         lhsT=w1_perm[e][:, 256 * j : 256 * (j + 1)].bitcast(FP4X4),
-                        lhsT_scale=(s1_perm[:] if e == 0 else s1_low[:, e - 1, :])[:, 128 * j : 128 * (j + 1)],
+                        lhsT_scale=s1_perm[:, H * e + 128 * j : H * e + 128 * (j + 1)],
                         rhs=x_codes[2 * e + b].bitcast(FP8X4),
                         rhs_scale=x_scales[2 * e + b],
                         start=True,

@@ -11,38 +11,55 @@ U8 = mybir.dt.uint8
 FP8X4 = mybir.dt.float8_e4m3fn_x4
 FP4X4 = mybir.dt.float4_e2m1fn_x4
 GELU = mybir.ActivationFunctionType.Gelu_apprx_tanh
+COPY = mybir.ActivationFunctionType.Copy
 MULT = mybir.AluOpType.mult
+ADD = mybir.AluOpType.add
 
 P = 128
 K, T, E, C, H, N = 512, 1536, 4, 256, 512, 128
 S = E * C
 FLOPS = 2 * S * (K * H + H * N)
 
+X_LOADS = [[(0, 896, 608), (896, 640, 208)], [(0, 768, 576), (768, 576, 224), (1344, 192, 48)]]
+SPLIT = 576
+STORES = [(a, a + 256) for a in range(0, T, 256)]
+
 
 def tile_moe_two_mlp_gelu_kernel(tc, xT, w1_words, w1_scales, w2_words, w2_scales, gate, offs, dst, out):
     nc = tc.nc
     with ExitStack() as ctx:
         keep = ctx.enter_context(tc.tile_pool(name="keep", bufs=1))
-        shared = ctx.enter_context(tc.tile_pool(name="shared", bufs=1))
         late = ctx.enter_context(tc.tile_pool(name="late", bufs=1))
-        ps_a = ctx.enter_context(tc.psum_pool(name="ps_a", bufs=6))
-        ps_y = ctx.enter_context(tc.psum_pool(name="ps_y", bufs=2))
+        ps_a = ctx.enter_context(tc.psum_pool(name="ps_a", bufs=5))
+        ps_y = ctx.enter_context(tc.psum_pool(name="ps_y", bufs=3))
 
         offs_t = keep.tile([P, S // 16], U16, name="offs_t")
         dst_t = keep.tile([P, S // 16], U16, name="dst_t")
         s1_raw = keep.tile([P, E * H], U8, name="s1_raw", align_bytes=64)
-        s1_perm = keep.tile([P, E * (H + N)], U8, name="s1_perm", align_bytes=64)
-        s2_t = s1_perm[:, E * H :].rearrange("p (e i) -> p e i", e=E)
-        placed = keep.tile([P, T], F32, name="placed")
+        w_scales = keep.tile([P, E * (H + N)], U8, name="w_scales", align_bytes=64)
+        placed_v = keep.tile([P, T], F32, name="placed_v")
+        placed_s = keep.tile([P, T], F32, name="placed_s")
         warm = keep.tile([P, 1], F32, name="warm")
 
         nc.gpsimd.memset(s1_raw[:].bitcast(I32), 0)
         nc.vector.memset(warm[:], 0.0)
         nc.scalar.activation(out=warm[:], in_=warm[:], func=GELU)
-        nc.gpsimd.memset(s1_perm[:, E * H :].bitcast(I32), 0)
-        nc.gpsimd.memset(placed[:], 0.0)
+        nc.gpsimd.memset(w_scales[:, E * H :].bitcast(I32), 0)
+        nc.gpsimd.memset(placed_v[:], 0.0)
+        nc.vector.memset(placed_s[:], 0.0)
 
-        w1_raw, w1_perm = {}, {}
+        x_rows = xT.rearrange("(p h j) t -> h p j t", h=2, j=2)
+        x_raw = {}
+
+        def load_x(h, c):
+            t0, n = X_LOADS[h][c][:2]
+            if (h, c) == (1, 2):
+                x_raw[h, c] = late.tile([P, 2, n], F32, name="x_raw%d_%d" % (h, c), align_bytes=64, offset=0)
+            else:
+                x_raw[h, c] = keep.tile([P, 2, n], F32, name="x_raw%d_%d" % (h, c))
+            nc.sync.dma_start(out=x_raw[h, c][:], in_=x_rows[h, :, :, t0 : t0 + n])
+
+        w1_raw = {}
 
         def load_w1(e0, e1):
             raw = keep.tile([P, (e1 - e0) * 2 * H], U8, name="w1_raw%d" % e0, align_bytes=64)
@@ -53,223 +70,168 @@ def tile_moe_two_mlp_gelu_kernel(tc, xT, w1_words, w1_scales, w2_words, w2_scale
             for e in range(e0, e1):
                 w1_raw[e] = raw[:, 2 * H * (e - e0) : 2 * H * (e - e0 + 1)]
 
-        def load_packed_scales():
-            nc.sync.dma_start(
-                out=s1_raw[0:P:8, :].rearrange("q (e i) -> q e i", e=E).bitcast(I32),
-                in_=w1_scales[:, 0].rearrange("e q i -> q e i").bitcast(I32),
-            )
+        load_x(0, 0)
+        nc.sync.dma_start(
+            out=s1_raw[0:P:8, :].rearrange("q (e i) -> q e i", e=E).bitcast(I32),
+            in_=w1_scales[:, 0].rearrange("e q i -> q e i").bitcast(I32),
+        )
+        load_x(0, 1)
+        nc.sync.dma_start(offs_t[:], offs)
+        nc.sync.dma_start(
+            out=w_scales[0:P:8, E * H :].rearrange("q (e i) -> q e i", e=E).bitcast(I32),
+            in_=w2_scales[:, 0].rearrange("e q i -> q e i").bitcast(I32),
+        )
+        for c in range(len(X_LOADS[1])):
+            load_x(1, c)
+        nc.vector.tensor_copy(
+            out=w_scales[:, : E * H].rearrange("p (e j c) -> p e j c", e=E, j=4),
+            in_=s1_raw[:].rearrange("p (e c j) -> p e j c", e=E, j=4),
+        )
+        load_w1(0, 1)
+        load_w1(1, 2)
+        for r in range(1, 4):
+            nc.sync.dma_start(out=w_scales[r:P:32, :].bitcast(I32), in_=w_scales[8 * r : P : 32, :].bitcast(I32))
+        load_w1(2, E)
+        nc.sync.dma_start(dst_t[:], dst)
 
-        def load_second_scales():
-            nc.sync.dma_start(
-                out=s1_perm[0:P:8, E * H :].rearrange("q (e i) -> q e i", e=E).bitcast(I32),
-                in_=w2_scales[:, 0].rearrange("e q i -> q e i").bitcast(I32),
-            )
+        pairs = [keep.tile([P, T, 2], BF16, name="pairs%d" % h, align_bytes=64) for h in range(2)]
+        picked = keep.tile([P, 6, C], U32, name="picked", align_bytes=64)
+        first_row = [2, 3, 1, 0]
+        second_row = [4, 5, 2, 1]
 
-        def lower_scales(r):
-            nc.sync.dma_start(
-                out=s1_perm[r:P:32, :].bitcast(I32),
-                in_=s1_perm[8 * r : P : 32, :].bitcast(I32),
-            )
+        def round_x(h):
+            for c, (t0, n, share) in enumerate(X_LOADS[h]):
+                for engine_copy, a, b in ((nc.scalar.copy, 0, share), (nc.vector.tensor_copy, share, n)):
+                    engine_copy(
+                        out=pairs[h][:, t0 + a : t0 + b, :],
+                        in_=x_raw[h, c][:, :, a:b].rearrange("p j t -> p t j"),
+                    )
 
-        def permute_words(e):
-            w1_perm[e] = keep.tile([P, 2 * H], U8, name="w1_perm%d" % e, align_bytes=64)
+        def gather(h, row, s0, n):
             nc.vector.tensor_copy(
+                out=picked[:].rearrange("p r s -> p (r s)")[:, row * C : row * C + n],
+                in_=pairs[h][:].rearrange("p t j -> p (t j)").bitcast(U32).indirect(offs_t[:, s0 // 16 : (s0 + n) // 16]),
+            )
+
+        grouped, w1_perm, x_codes, x_scales, h_raw, h_codes, h_scales, y_ps = {}, {}, {}, {}, {}, {}, {}, {}
+
+        def weave(e, engine_copy, dtype, a, b):
+            if e not in grouped:
+                grouped[e] = keep.tile([P, C, 4], BF16, name="grouped%d" % e, align_bytes=64, tag="grouped%d" % min(e, 1))
+            r0, r1 = first_row[e], second_row[e]
+            words = grouped[e][:].rearrange("p s j -> p (s j)").bitcast(dtype).rearrange("p (s h) -> p s h", h=2)
+            both = picked[:].bitcast(dtype)[:, r0 : r1 + 1 : r1 - r0, a:b]
+            engine_copy(out=words[:, a:b, :], in_=both.rearrange("p h s -> p s h"))
+
+        def permute(e, engine_copy):
+            w1_perm[e] = keep.tile([P, 2 * H], U8, name="w1_perm%d" % e, align_bytes=64, tag="w1_perm%d" % (e % 3))
+            engine_copy(
                 out=w1_perm[e][:].bitcast(U16).rearrange("p (j c) -> p j c", j=4),
                 in_=w1_raw[e].bitcast(U16).rearrange("p (c j) -> p j c", j=4),
             )
 
-        def permute_scales():
-            nc.vector.tensor_copy(
-                out=s1_perm[:, : E * H].rearrange("p (e j c) -> p e j c", e=E, j=4),
-                in_=s1_raw[:].rearrange("p (e m j) -> p e j m", e=E, j=4),
-            )
-
-        pairs = [keep.tile([P, T, 2], BF16, name="pairs%d" % h, align_bytes=64) for h in range(2)]
-        grouped = keep.tile([P, S, 4], BF16, name="grouped", align_bytes=64)
-        picked = keep.tile([P, 3, S // 2], U32, name="picked", align_bytes=64)
-        x_rows = xT.rearrange("(p h j) t -> h p j t", h=2, j=2)
-        chunks = [[(0, 896), (896, 640)], [(0, 768), (768, 576), (1344, 192)]]
-        x_raw = {}
-
-        def load_x(h, c):
-            t0, n = chunks[h][c]
-            if (h, c) == (1, 2):
-                x_raw[h, c] = late.tile([P, 2, n], F32, name="x_raw%d_%d" % (h, c), align_bytes=64, offset=0)
-            else:
-                x_raw[h, c] = keep.tile([P, 2, n], F32, name="x_raw%d_%d" % (h, c))
-            nc.sync.dma_start(out=x_raw[h, c][:], in_=x_rows[h, :, :, t0 : t0 + n])
-
-        load_x(0, 0)
-        load_packed_scales()
-        load_x(0, 1)
-        nc.sync.dma_start(offs_t[:], offs)
-        load_second_scales()
-        for c in range(3):
-            load_x(1, c)
-        permute_scales()
-        load_w1(0, 2)
-        for r in range(1, 4):
-            lower_scales(r)
-        load_w1(2, 4)
-        nc.sync.dma_start(dst_t[:], dst)
-
-        def pair(engine_copy, h, c, a, n):
-            t0 = chunks[h][c][0]
-            engine_copy(
-                out=pairs[h][:, t0 + a : t0 + a + n, :],
-                in_=x_raw[h, c][:, :, a : a + n].rearrange("p j t -> p t j"),
-            )
-
-        sc, ve = nc.scalar.copy, nc.vector.tensor_copy
-        slot_words = grouped[:].rearrange("p s j -> p (s j)").bitcast(U32).rearrange("p (s h) -> p s h", h=2)
-
-        def gather(out_words, h, s0, n):
-            nc.vector.tensor_copy(
-                out=out_words,
-                in_=pairs[h][:].rearrange("p t j -> p (t j)").bitcast(U32).indirect(offs_t[:, s0 // 16 : (s0 + n) // 16]),
-            )
-
-        def pick(s0, n):
-            gather(picked[:, 2, s0 % 512 : s0 % 512 + n], 1, s0, n)
-
-        views = {
-            U32: (picked[:], slot_words),
-            I32: (
-                picked[:].bitcast(I32),
-                grouped[:].rearrange("p s j -> p (s j)").bitcast(I32).rearrange("p (s h) -> p s h", h=2),
-            ),
-        }
-
-        def weave(engine_copy, dtype, s0, n):
-            row = s0 // 512
-            source, target = views[dtype]
-            both = source[:, row : 3 : 2 - row, s0 % 512 : s0 % 512 + n]
-            engine_copy(out=target[:, s0 : s0 + n, :], in_=both.rearrange("p h s -> p s h"))
-
-        pair(sc, 0, 0, 0, 608)
-        pair(ve, 0, 0, 608, 288)
-        pair(sc, 0, 1, 0, 208)
-        pair(ve, 0, 1, 208, 432)
-        gather(picked[:, 0:2, :].rearrange("p r s -> p (r s)"), 0, 0, S)
-        pair(sc, 1, 0, 0, 576)
-        pair(ve, 1, 0, 576, 192)
-        pair(sc, 1, 1, 0, 224)
-        pair(ve, 1, 1, 224, 352)
-        pair(sc, 1, 2, 0, 48)
-        pair(ve, 1, 2, 48, 144)
-        w2_t = late.tile([P, E, 2 * N], U8, name="w2_t", align_bytes=64, offset=0)
-        gate_t = late.tile([P, S], F32, name="gate_t", align_bytes=64, offset=E * 2 * N)
-        nc.scalar.dma_start(out=w2_t[:].bitcast(I32), in_=w2_words[:, 0].rearrange("e p b -> p e b").bitcast(I32))
-        nc.scalar.dma_start(out=gate_t[:], in_=gate)
-
-        x_codes, x_scales = {}, {}
-        h_raw, h_codes, h_scales, y_raw = {}, {}, {}, {}
-        pieces = [[(0, 128), (128, 256)]] + [[(0, 256)]] * (E - 1)
-
-        def quant_x(s0, n):
-            codes = keep.tile([P, n], U32, name="x_codes%d" % s0, align_bytes=64)
-            if s0 >= 2 * C:
-                scales = shared.tile([P, n], U8, name="x_scales%d" % s0, align_bytes=64, offset=2 * H + s0 - 2 * C)
-            else:
-                scales = keep.tile([P, n], U8, name="x_scales%d" % s0, align_bytes=64)
+        def quant_x(e, a, b):
+            if e not in x_codes:
+                x_codes[e] = keep.tile([P, C], U32, name="x_codes%d" % e, align_bytes=64, tag="x_codes%d" % e)
+                x_scales[e] = keep.tile([P, C], U8, name="x_scales%d" % e, align_bytes=64)
             nc.vector.quantize_mx(
-                out=codes[:].bitcast(FP8X4),
-                scales=scales[:],
-                in_=grouped[:, s0 : s0 + n, :].rearrange("p s j -> p (s j)"),
+                out=x_codes[e][:, a:b].bitcast(FP8X4),
+                scales=x_scales[e][:, a:b],
+                in_=grouped[e][:, a:b, :].rearrange("p s j -> p (s j)"),
             )
-            for b in range(n // 128):
-                x_codes[s0 // 128 + b] = codes[:, 128 * b : 128 * (b + 1)]
-                x_scales[s0 // 128 + b] = scales[:, 128 * b : 128 * (b + 1)]
 
         def layer1(e):
-            if e == 0:
-                h_raw[e] = shared.tile([P, C, 4], BF16, name="h_raw%d" % e, align_bytes=64, offset=0)
-            else:
-                h_raw[e] = keep.tile([P, C, 4], BF16, name="h_raw%d" % e, align_bytes=64, tag="h%d" % e)
-            for b in range(2):
+            h_raw[e] = keep.tile([P, C, 4], BF16, name="h_raw%d" % e, align_bytes=64)
+            for a in (0, 128):
                 acc = ps_a.tile([P, 4, 128], F32, name="acc")
                 for j in range(4):
                     nc.tensor.matmul_mx(
                         out=acc[:, j, :],
                         lhsT=w1_perm[e][:, 256 * j : 256 * (j + 1)].bitcast(FP4X4),
-                        lhsT_scale=s1_perm[:, H * e + 128 * j : H * e + 128 * (j + 1)],
-                        rhs=x_codes[2 * e + b].bitcast(FP8X4),
-                        rhs_scale=x_scales[2 * e + b],
+                        lhsT_scale=w_scales[:, H * e + 128 * j : H * e + 128 * (j + 1)],
+                        rhs=x_codes[e][:, a : a + 128].bitcast(FP8X4),
+                        rhs_scale=x_scales[e][:, a : a + 128],
                         start=True,
                         stop=True,
                     )
-                nc.scalar.activation(
-                    out=h_raw[e][:, 128 * b : 128 * (b + 1), :],
-                    in_=acc[:].rearrange("p j s -> p s j"),
-                    func=GELU,
-                )
-
-        def quant_h(e):
-            h_codes[e] = keep.tile([P, C], U32, name="h_codes%d" % e, align_bytes=64, tag="h2" if e == 0 else "h_codes%d" % e)
-            h_scales[e] = keep.tile([P, C], U8, name="h_scales%d" % e, align_bytes=64)
-            for s0, s1 in pieces[e]:
-                nc.vector.quantize_mx(
-                    out=h_codes[e][:, s0:s1].bitcast(FP8X4),
-                    scales=h_scales[e][:, s0:s1],
-                    in_=h_raw[e][:, s0:s1, :].rearrange("p s j -> p (s j)"),
-                )
+                nc.scalar.activation(out=h_raw[e][:, a : a + 128, :], in_=acc[:].rearrange("p j s -> p s j"), func=GELU)
 
         def layer2(e):
-            y_raw[e] = keep.tile([P, C], F32, name="y_raw%d" % e)
-            for s0, s1 in pieces[e]:
-                y_ps = ps_y.tile([P, s1 - s0], F32, name="y_ps")
-                nc.tensor.matmul_mx(
-                    out=y_ps[:],
-                    lhsT=w2_t[:, e, :].bitcast(FP4X4),
-                    lhsT_scale=s2_t[:, e, :],
-                    rhs=h_codes[e][:, s0:s1].bitcast(FP8X4),
-                    rhs_scale=h_scales[e][:, s0:s1],
-                    start=True,
-                    stop=True,
-                )
-                nc.scalar.copy(out=y_raw[e][:, s0:s1], in_=y_ps[:])
-
-        def scatter(e):
-            nc.vector.tensor_tensor(
-                placed[:].indirect(dst_t[:, 16 * e : 16 * (e + 1)]),
-                y_raw[e][:],
-                gate_t[:, C * e : C * (e + 1)],
-                MULT,
+            h_codes[e] = keep.tile([P, C], U32, name="h_codes%d" % e, align_bytes=64)
+            h_scales[e] = keep.tile([P, C], U8, name="h_scales%d" % e, align_bytes=64)
+            nc.vector.quantize_mx(
+                out=h_codes[e][:].bitcast(FP8X4),
+                scales=h_scales[e][:],
+                in_=h_raw[e][:].rearrange("p s j -> p (s j)"),
+            )
+            y_ps[e] = ps_y.tile([P, C], F32, name="y_ps")
+            nc.tensor.matmul_mx(
+                out=y_ps[e][:],
+                lhsT=w2_t[:, e, :].bitcast(FP4X4),
+                lhsT_scale=w_scales[:, E * H + N * e : E * H + N * (e + 1)],
+                rhs=h_codes[e][:].bitcast(FP8X4),
+                rhs_scale=h_scales[e][:],
+                start=True,
+                stop=True,
             )
 
-        pick(0, 256)
-        weave(sc, U32, 0, 128)
-        weave(sc, U32, 128, 128)
-        pick(256, 256)
-        weave(sc, U32, 256, 256)
-        permute_words(0)
-        quant_x(0, 128)
-        quant_x(128, 128)
+        def weigh(target, s0, s1):
+            e = s0 // C
+            nc.vector.tensor_tensor(target, y_ps[e][:, s0 - C * e : s1 - C * e], gate_t[:, s0:s1], MULT)
+
+        def places(window, s0, s1):
+            return window[:].indirect(dst_t[:, s0 // 16 : s1 // 16])
+
+        round_x(0)
+        gather(0, first_row[0], 0, 2 * C)
+        gather(0, first_row[2], 2 * C, C)
+        gather(0, first_row[3], 3 * C, C)
+        round_x(1)
+        w2_t = late.tile([P, E, 2 * N], U8, name="w2_t", align_bytes=64, offset=0)
+        gate_t = late.tile([P, S], F32, name="gate_t", align_bytes=64, offset=E * 2 * N)
+        nc.sync.dma_start(out=w2_t[:].bitcast(I32), in_=w2_words[:, 0].rearrange("e p b -> p e b").bitcast(I32))
+        nc.sync.dma_start(out=gate_t[:], in_=gate)
+
+        gather(1, second_row[0], 0, C)
+        gather(1, second_row[1], C, C)
+        permute(0, nc.scalar.copy)
+        weave(0, nc.scalar.copy, U32, 0, 128)
+        weave(0, nc.scalar.copy, U32, 128, C)
+        weave(1, nc.scalar.copy, U32, 0, C)
+        permute(1, nc.scalar.copy)
+        quant_x(0, 0, 128)
+        quant_x(0, 128, C)
         layer1(0)
-        permute_words(1)
-        quant_x(256, 128)
-        quant_x(384, 128)
+        gather(1, second_row[2], 2 * C, C)
+        permute(2, nc.vector.tensor_copy)
+        quant_x(1, 0, C)
         layer1(1)
-        pick(512, 512)
-        weave(ve, I32, 512, 512)
-        quant_h(0)
-        layer2(0)
-        permute_words(2)
-        quant_x(512, 128)
-        quant_x(640, 128)
-        permute_words(3)
-        quant_x(768, 256)
-        quant_h(1)
-        scatter(0)
+        weave(2, nc.vector.tensor_copy, I32, 0, C)
+        gather(1, second_row[3], 3 * C, C)
+        quant_x(2, 0, C)
         layer1(2)
-        layer2(1)
-        quant_h(2)
-        scatter(1)
+        weave(3, nc.vector.tensor_copy, I32, 0, C)
+        permute(3, nc.vector.tensor_copy)
+        quant_x(3, 0, C)
         layer1(3)
+        y_first = keep.tile([P, C], F32, name="y_first", align_bytes=64, tag="x_codes3")
+        y_second = keep.tile([P, SPLIT - C], F32, name="y_second")
+        y_third = keep.tile([P, 3 * C - SPLIT], F32, name="y_third")
+        y_last = keep.tile([P, C], F32, name="y_last")
+        layer2(0)
+        layer2(1)
+        weigh(y_first[:], 0, C)
         layer2(2)
-        quant_h(3)
-        scatter(2)
+        weigh(y_second[:, :C], C, 2 * C)
         layer2(3)
-        scatter(3)
-        nc.sync.dma_start(out=out[:, : T // 2], in_=placed[:, : T // 2])
-        nc.scalar.dma_start(out=out[:, T // 2 :], in_=placed[:, T // 2 :])
+        nc.scalar.copy(out=y_third[:], in_=y_ps[2][:, SPLIT - 2 * C :])
+        weigh(y_second[:, C:], 2 * C, SPLIT)
+        nc.scalar.activation(places(placed_s, 0, C), y_first[:], COPY)
+        nc.vector.tensor_tensor(places(placed_v, SPLIT, 3 * C), y_third[:], gate_t[:, SPLIT : 3 * C], MULT)
+        weigh(y_last[:], 3 * C, S)
+        nc.scalar.activation(places(placed_s, C, SPLIT), y_second[:], COPY)
+        nc.vector.tensor_copy(places(placed_v, 3 * C, S), y_last[:])
+        for k, (a, b) in enumerate(STORES):
+            nc.vector.tensor_tensor(placed_v[:, a:b], placed_v[:, a:b], placed_s[:, a:b], ADD)
+            queue = nc.sync if k % 2 == 0 else nc.scalar
+            queue.dma_start(out=out[:, a:b], in_=placed_v[:, a:b])

@@ -22,7 +22,7 @@ FLOPS = 2 * S * (K * H + H * N)
 
 X_LOADS = [[(0, 896, 608), (896, 640, 208)], [(0, 768, 576), (768, 576, 224), (1344, 192, 48)]]
 SPLIT = 576
-STORES = [(a, a + 256) for a in range(0, T, 256)]
+STORES = [(0, T // 2), (T // 2, T)]
 
 
 def tile_moe_two_mlp_gelu_kernel(tc, xT, w1_words, w1_scales, w2_words, w2_scales, gate, offs, dst, out):

@@ -31,7 +31,7 @@ def tile_moe_two_mlp_gelu_kernel(tc, xT, w1_words, w1_scales, w2_words, w2_scale
         keep = ctx.enter_context(tc.tile_pool(name="keep", bufs=1))
         late = ctx.enter_context(tc.tile_pool(name="late", bufs=1))
         ps_a = ctx.enter_context(tc.psum_pool(name="ps_a", bufs=5))
-        ps_y = ctx.enter_context(tc.psum_pool(name="ps_y", bufs=3))
+        ps_y = ctx.enter_context(tc.psum_pool(name="ps_y", bufs=1))
 
         offs_t = keep.tile([P, S // 16], U16, name="offs_t")
         dst_t = keep.tile([P, S // 16], U16, name="dst_t")
@@ -39,14 +39,13 @@ def tile_moe_two_mlp_gelu_kernel(tc, xT, w1_words, w1_scales, w2_words, w2_scale
         w_scales = keep.tile([P, E * (H + N)], U8, name="w_scales", align_bytes=64)
         placed_v = keep.tile([P, T], F32, name="placed_v")
         placed_s = keep.tile([P, T], F32, name="placed_s")
-        warm = keep.tile([P, 1], F32, name="warm")
+        zero = keep.tile([P, 1], F32, name="zero")
 
+        nc.gpsimd.memset(zero[:], 0.0)
         nc.gpsimd.memset(s1_raw[:].bitcast(I32), 0)
-        nc.vector.memset(warm[:], 0.0)
-        nc.scalar.activation(out=warm[:], in_=warm[:], func=GELU)
+        nc.scalar.activation(out=placed_s[:], in_=zero[:].to_broadcast([P, T]), func=GELU)
         nc.gpsimd.memset(w_scales[:, E * H :].bitcast(I32), 0)
         nc.gpsimd.memset(placed_v[:], 0.0)
-        nc.vector.memset(placed_s[:], 0.0)
 
         x_rows = xT.rearrange("(p h j) t -> h p j t", h=2, j=2)
         x_raw = {}
@@ -96,8 +95,8 @@ def tile_moe_two_mlp_gelu_kernel(tc, xT, w1_words, w1_scales, w2_words, w2_scale
 
         pairs = [keep.tile([P, T, 2], BF16, name="pairs%d" % h, align_bytes=64) for h in range(2)]
         picked = keep.tile([P, 6, C], U32, name="picked", align_bytes=64)
-        first_row = [2, 3, 1, 0]
-        second_row = [4, 5, 2, 1]
+        first_row = [2, 3, 0, 1]
+        second_row = [4, 5, 2, 3]
 
         def round_x(h):
             for c, (t0, n, share) in enumerate(X_LOADS[h]):
@@ -113,7 +112,7 @@ def tile_moe_two_mlp_gelu_kernel(tc, xT, w1_words, w1_scales, w2_words, w2_scale
                 in_=pairs[h][:].rearrange("p t j -> p (t j)").bitcast(U32).indirect(offs_t[:, s0 // 16 : (s0 + n) // 16]),
             )
 
-        grouped, w1_perm, x_codes, x_scales, h_raw, h_codes, h_scales, y_ps = {}, {}, {}, {}, {}, {}, {}, {}
+        grouped, w1_perm, x_codes, x_scales, h_raw, h_codes, h_scales = {}, {}, {}, {}, {}, {}, {}
 
         def weave(e, engine_copy, dtype, a, b):
             if e not in grouped:
@@ -164,7 +163,6 @@ def tile_moe_two_mlp_gelu_kernel(tc, xT, w1_words, w1_scales, w2_words, w2_scale
                 scales=h_scales[e][:],
                 in_=h_raw[e][:].rearrange("p s j -> p (s j)"),
             )
-            y_ps[e] = ps_y.tile([P, C], F32, name="y_ps")
             nc.tensor.matmul_mx(
                 out=y_ps[e][:],
                 lhsT=w2_t[:, e, :].bitcast(FP4X4),
@@ -175,17 +173,15 @@ def tile_moe_two_mlp_gelu_kernel(tc, xT, w1_words, w1_scales, w2_words, w2_scale
                 stop=True,
             )
 
-        def weigh(target, s0, s1):
-            e = s0 // C
-            nc.vector.tensor_tensor(target, y_ps[e][:, s0 - C * e : s1 - C * e], gate_t[:, s0:s1], MULT)
+        def weigh(target, sums, s0, s1):
+            nc.vector.tensor_tensor(target, sums, gate_t[:, s0:s1], MULT)
 
         def places(window, s0, s1):
             return window[:].indirect(dst_t[:, s0 // 16 : s1 // 16])
 
         round_x(0)
         gather(0, first_row[0], 0, 2 * C)
-        gather(0, first_row[2], 2 * C, C)
-        gather(0, first_row[3], 3 * C, C)
+        gather(0, first_row[2], 2 * C, 2 * C)
         round_x(1)
         w2_t = late.tile([P, E, 2 * N], U8, name="w2_t", align_bytes=64, offset=0)
         gate_t = late.tile([P, S], F32, name="gate_t", align_bytes=64, offset=E * 2 * N)
@@ -218,17 +214,18 @@ def tile_moe_two_mlp_gelu_kernel(tc, xT, w1_words, w1_scales, w2_words, w2_scale
         y_second = keep.tile([P, SPLIT - C], F32, name="y_second")
         y_third = keep.tile([P, 3 * C - SPLIT], F32, name="y_third")
         y_last = keep.tile([P, C], F32, name="y_last")
+        y_ps = [ps_y.tile([P, C], F32, name="y_ps%d" % e, tag="y_ps%d" % (e % 3)) for e in range(E)]
         layer2(0)
         layer2(1)
-        weigh(y_first[:], 0, C)
+        weigh(y_first[:], y_ps[0][:], 0, C)
         layer2(2)
-        weigh(y_second[:, :C], C, 2 * C)
+        weigh(y_second[:, :C], y_ps[1][:], C, 2 * C)
         layer2(3)
         nc.scalar.copy(out=y_third[:], in_=y_ps[2][:, SPLIT - 2 * C :])
-        weigh(y_second[:, C:], 2 * C, SPLIT)
+        weigh(y_second[:, C:], y_ps[2][:, : SPLIT - 2 * C], 2 * C, SPLIT)
         nc.scalar.activation(places(placed_s, 0, C), y_first[:], COPY)
         nc.vector.tensor_tensor(places(placed_v, SPLIT, 3 * C), y_third[:], gate_t[:, SPLIT : 3 * C], MULT)
-        weigh(y_last[:], 3 * C, S)
+        weigh(y_last[:], y_ps[3][:], 3 * C, S)
         nc.scalar.activation(places(placed_s, C, SPLIT), y_second[:], COPY)
         nc.vector.tensor_copy(places(placed_v, 3 * C, S), y_last[:])
         for k, (a, b) in enumerate(STORES):

@@ -20,9 +20,9 @@ K, T, E, C, H, N = 512, 1536, 4, 256, 512, 128
 S = E * C
 FLOPS = 2 * S * (K * H + H * N)
 
-X_LOADS = [[(0, 896, 608), (896, 640, 208)], [(0, 768, 576), (768, 576, 224), (1344, 192, 48)]]
-SPLIT = 576
-STORES = [(0, T // 2), (T // 2, T)]
+X_LOADS = [[(0, 768, 768), (768, 768, 288)], [(0, 512, 512), (512, 832, 448), (1344, 192, 0)]]
+CUTS = (0, 384, 576, 800, S)
+STORES = [(a, a + 512) for a in range(0, T, 512)]
 
 
 def tile_moe_two_mlp_gelu_kernel(tc, xT, w1_words, w1_scales, w2_words, w2_scales, gate, offs, dst, out):
@@ -30,8 +30,7 @@ def tile_moe_two_mlp_gelu_kernel(tc, xT, w1_words, w1_scales, w2_words, w2_scale
     with ExitStack() as ctx:
         keep = ctx.enter_context(tc.tile_pool(name="keep", bufs=1))
         late = ctx.enter_context(tc.tile_pool(name="late", bufs=1))
-        ps_a = ctx.enter_context(tc.psum_pool(name="ps_a", bufs=5))
-        ps_y = ctx.enter_context(tc.psum_pool(name="ps_y", bufs=1))
+        psum = ctx.enter_context(tc.psum_pool(name="psum", bufs=1))
 
         offs_t = keep.tile([P, S // 16], U16, name="offs_t")
         dst_t = keep.tile([P, S // 16], U16, name="dst_t")
@@ -87,10 +86,9 @@ def tile_moe_two_mlp_gelu_kernel(tc, xT, w1_words, w1_scales, w2_words, w2_scale
             in_=s1_raw[:].rearrange("p (e c j) -> p e j c", e=E, j=4),
         )
         load_w1(0, 1)
-        load_w1(1, 2)
+        load_w1(1, E)
         for r in range(1, 4):
             nc.sync.dma_start(out=w_scales[r:P:32, :].bitcast(I32), in_=w_scales[8 * r : P : 32, :].bitcast(I32))
-        load_w1(2, E)
         nc.sync.dma_start(dst_t[:], dst)
 
         pairs = [keep.tile([P, T, 2], BF16, name="pairs%d" % h, align_bytes=64) for h in range(2)]
@@ -101,10 +99,11 @@ def tile_moe_two_mlp_gelu_kernel(tc, xT, w1_words, w1_scales, w2_words, w2_scale
         def round_x(h):
             for c, (t0, n, share) in enumerate(X_LOADS[h]):
                 for engine_copy, a, b in ((nc.scalar.copy, 0, share), (nc.vector.tensor_copy, share, n)):
-                    engine_copy(
-                        out=pairs[h][:, t0 + a : t0 + b, :],
-                        in_=x_raw[h, c][:, :, a:b].rearrange("p j t -> p t j"),
-                    )
+                    if a < b:
+                        engine_copy(
+                            out=pairs[h][:, t0 + a : t0 + b, :],
+                            in_=x_raw[h, c][:, :, a:b].rearrange("p j t -> p t j"),
+                        )
 
         def gather(h, row, s0, n):
             nc.vector.tensor_copy(
@@ -112,18 +111,18 @@ def tile_moe_two_mlp_gelu_kernel(tc, xT, w1_words, w1_scales, w2_words, w2_scale
                 in_=pairs[h][:].rearrange("p t j -> p (t j)").bitcast(U32).indirect(offs_t[:, s0 // 16 : (s0 + n) // 16]),
             )
 
-        grouped, w1_perm, x_codes, x_scales, h_raw, h_codes, h_scales = {}, {}, {}, {}, {}, {}, {}
+        grouped, w1_perm, x_codes, x_scales, h_raw, h_codes, h_scales, y_ps = {}, {}, {}, {}, {}, {}, {}, {}
 
         def weave(e, engine_copy, dtype, a, b):
             if e not in grouped:
-                grouped[e] = keep.tile([P, C, 4], BF16, name="grouped%d" % e, align_bytes=64, tag="grouped%d" % min(e, 1))
+                grouped[e] = keep.tile([P, C, 4], BF16, name="grouped%d" % e, align_bytes=64, tag="grouped%d" % e)
             r0, r1 = first_row[e], second_row[e]
             words = grouped[e][:].rearrange("p s j -> p (s j)").bitcast(dtype).rearrange("p (s h) -> p s h", h=2)
             both = picked[:].bitcast(dtype)[:, r0 : r1 + 1 : r1 - r0, a:b]
             engine_copy(out=words[:, a:b, :], in_=both.rearrange("p h s -> p s h"))
 
         def permute(e, engine_copy):
-            w1_perm[e] = keep.tile([P, 2 * H], U8, name="w1_perm%d" % e, align_bytes=64, tag="w1_perm%d" % (e % 3))
+            w1_perm[e] = keep.tile([P, 2 * H], U8, name="w1_perm%d" % e, align_bytes=64, tag=("w1_perm0", "w1_perm1", "grouped0", "grouped2")[e])
             engine_copy(
                 out=w1_perm[e][:].bitcast(U16).rearrange("p (j c) -> p j c", j=4),
                 in_=w1_raw[e].bitcast(U16).rearrange("p (c j) -> p j c", j=4),
@@ -142,7 +141,7 @@ def tile_moe_two_mlp_gelu_kernel(tc, xT, w1_words, w1_scales, w2_words, w2_scale
         def layer1(e):
             h_raw[e] = keep.tile([P, C, 4], BF16, name="h_raw%d" % e, align_bytes=64)
             for a in (0, 128):
-                acc = ps_a.tile([P, 4, 128], F32, name="acc")
+                acc = psum.tile([P, 4, 128], F32, name="acc", tag="bank%d" % ((2 * e + a // 128) % 5))
                 for j in range(4):
                     nc.tensor.matmul_mx(
                         out=acc[:, j, :],
@@ -163,6 +162,7 @@ def tile_moe_two_mlp_gelu_kernel(tc, xT, w1_words, w1_scales, w2_words, w2_scale
                 scales=h_scales[e][:],
                 in_=h_raw[e][:].rearrange("p s j -> p (s j)"),
             )
+            y_ps[e] = psum.tile([P, C], F32, name="y_ps%d" % e, tag="bank%d" % (5, 6, 1, 7)[e])
             nc.tensor.matmul_mx(
                 out=y_ps[e][:],
                 lhsT=w2_t[:, e, :].bitcast(FP4X4),
@@ -173,8 +173,8 @@ def tile_moe_two_mlp_gelu_kernel(tc, xT, w1_words, w1_scales, w2_words, w2_scale
                 stop=True,
             )
 
-        def weigh(target, sums, s0, s1):
-            nc.vector.tensor_tensor(target, sums, gate_t[:, s0:s1], MULT)
+        def weigh(e):
+            nc.vector.tensor_tensor(y[:, C * e : C * (e + 1)], y_ps[e][:], gate_t[:, C * e : C * (e + 1)], MULT)
 
         def places(window, s0, s1):
             return window[:].indirect(dst_t[:, s0 // 16 : s1 // 16])
@@ -210,24 +210,20 @@ def tile_moe_two_mlp_gelu_kernel(tc, xT, w1_words, w1_scales, w2_words, w2_scale
         permute(3, nc.vector.tensor_copy)
         quant_x(3, 0, C)
         layer1(3)
-        y_first = keep.tile([P, C], F32, name="y_first", align_bytes=64, tag="x_codes3")
-        y_second = keep.tile([P, SPLIT - C], F32, name="y_second")
-        y_third = keep.tile([P, 3 * C - SPLIT], F32, name="y_third")
-        y_last = keep.tile([P, C], F32, name="y_last")
-        y_ps = [ps_y.tile([P, C], F32, name="y_ps%d" % e, tag="y_ps%d" % (e % 3)) for e in range(E)]
+        y = keep.tile([P, S], F32, name="y", align_bytes=64, tag="x_codes3")
         layer2(0)
         layer2(1)
-        weigh(y_first[:], y_ps[0][:], 0, C)
+        weigh(0)
         layer2(2)
-        weigh(y_second[:, :C], y_ps[1][:], C, 2 * C)
+        weigh(1)
+        weigh(2)
         layer2(3)
-        nc.scalar.copy(out=y_third[:], in_=y_ps[2][:, SPLIT - 2 * C :])
-        weigh(y_second[:, C:], y_ps[2][:, : SPLIT - 2 * C], 2 * C, SPLIT)
-        nc.scalar.activation(places(placed_s, 0, C), y_first[:], COPY)
-        nc.vector.tensor_tensor(places(placed_v, SPLIT, 3 * C), y_third[:], gate_t[:, SPLIT : 3 * C], MULT)
-        weigh(y_last[:], y_ps[3][:], 3 * C, S)
-        nc.scalar.activation(places(placed_s, C, SPLIT), y_second[:], COPY)
-        nc.vector.tensor_copy(places(placed_v, 3 * C, S), y_last[:])
+        cut = CUTS
+        nc.scalar.activation(places(placed_s, cut[0], cut[1]), y[:, cut[0] : cut[1]], COPY)
+        nc.vector.tensor_copy(places(placed_v, cut[1], cut[2]), y[:, cut[1] : cut[2]])
+        weigh(3)
+        nc.scalar.activation(places(placed_s, cut[2], cut[3]), y[:, cut[2] : cut[3]], COPY)
+        nc.vector.tensor_copy(places(placed_v, cut[3], cut[4]), y[:, cut[3] : cut[4]])
         for k, (a, b) in enumerate(STORES):
             nc.vector.tensor_tensor(placed_v[:, a:b], placed_v[:, a:b], placed_s[:, a:b], ADD)
             queue = nc.sync if k % 2 == 0 else nc.scalar

@@ -21,7 +21,7 @@ S = E * C
 FLOPS = 2 * S * (K * H + H * N)
 
 X_LOADS = [[(0, 768, 768), (768, 768, 288)], [(0, 512, 512), (512, 832, 448), (1344, 192, 0)]]
-CUTS = (0, 384, 576, 800, S)
+CUTS = (0, 192, 512, 768, S)
 STORES = [(a, a + 512) for a in range(0, T, 512)]
 
 
@@ -51,7 +51,7 @@ def tile_moe_two_mlp_gelu_kernel(tc, xT, w1_words, w1_scales, w2_words, w2_scale
 
         def load_x(h, c):
             t0, n = X_LOADS[h][c][:2]
-            if (h, c) == (1, 2):
+            if (h, c) == (1, len(X_LOADS[1]) - 1):
                 x_raw[h, c] = late.tile([P, 2, n], F32, name="x_raw%d_%d" % (h, c), align_bytes=64, offset=0)
             else:
                 x_raw[h, c] = keep.tile([P, 2, n], F32, name="x_raw%d_%d" % (h, c))
@@ -73,7 +73,8 @@ def tile_moe_two_mlp_gelu_kernel(tc, xT, w1_words, w1_scales, w2_words, w2_scale
             out=s1_raw[0:P:8, :].rearrange("q (e i) -> q e i", e=E).bitcast(I32),
             in_=w1_scales[:, 0].rearrange("e q i -> q e i").bitcast(I32),
         )
-        load_x(0, 1)
+        for c in range(1, len(X_LOADS[0])):
+            load_x(0, c)
         nc.sync.dma_start(offs_t[:], offs)
         nc.sync.dma_start(
             out=w_scales[0:P:8, E * H :].rearrange("q (e i) -> q e i", e=E).bitcast(I32),
@@ -107,11 +108,14 @@ def tile_moe_two_mlp_gelu_kernel(tc, xT, w1_words, w1_scales, w2_words, w2_scale
 
         def gather(h, row, s0, n):
             nc.vector.tensor_copy(
-                out=picked[:].rearrange("p r s -> p (r s)")[:, row * C : row * C + n],
+                out=picked[:].rearrange("p r s -> p (r s)")[:, row * C + s0 % C : row * C + s0 % C + n],
                 in_=pairs[h][:].rearrange("p t j -> p (t j)").bitcast(U32).indirect(offs_t[:, s0 // 16 : (s0 + n) // 16]),
             )
 
-        grouped, w1_perm, x_codes, x_scales, h_raw, h_codes, h_scales, y_ps = {}, {}, {}, {}, {}, {}, {}, {}
+        grouped, w1_perm, x_codes, x_scales = {}, {}, {}, {}
+        h_raw = keep.tile([P, S, 4], BF16, name="h_raw", align_bytes=64)
+        h_codes = keep.tile([P, S], U32, name="h_codes", align_bytes=64)
+        h_scales = keep.tile([P, S], U8, name="h_scales", align_bytes=64)
 
         def weave(e, engine_copy, dtype, a, b):
             if e not in grouped:
@@ -139,7 +143,6 @@ def tile_moe_two_mlp_gelu_kernel(tc, xT, w1_words, w1_scales, w2_words, w2_scale
             )
 
         def layer1(e):
-            h_raw[e] = keep.tile([P, C, 4], BF16, name="h_raw%d" % e, align_bytes=64)
             for a in (0, 128):
                 acc = psum.tile([P, 4, 128], F32, name="acc", tag="bank%d" % ((2 * e + a // 128) % 5))
                 for j in range(4):
@@ -152,29 +155,27 @@ def tile_moe_two_mlp_gelu_kernel(tc, xT, w1_words, w1_scales, w2_words, w2_scale
                         start=True,
                         stop=True,
                     )
-                nc.scalar.activation(out=h_raw[e][:, a : a + 128, :], in_=acc[:].rearrange("p j s -> p s j"), func=GELU)
+                nc.scalar.activation(out=h_raw[:, C * e + a : C * e + a + 128, :], in_=acc[:].rearrange("p j s -> p s j"), func=GELU)
 
-        def layer2(e):
-            h_codes[e] = keep.tile([P, C], U32, name="h_codes%d" % e, align_bytes=64)
-            h_scales[e] = keep.tile([P, C], U8, name="h_scales%d" % e, align_bytes=64)
+        def layer2(e, sums):
+            slots = slice(C * e, C * (e + 1))
             nc.vector.quantize_mx(
-                out=h_codes[e][:].bitcast(FP8X4),
-                scales=h_scales[e][:],
-                in_=h_raw[e][:].rearrange("p s j -> p (s j)"),
+                out=h_codes[:, slots].bitcast(FP8X4),
+                scales=h_scales[:, slots],
+                in_=h_raw[:, slots, :].rearrange("p s j -> p (s j)"),
             )
-            y_ps[e] = psum.tile([P, C], F32, name="y_ps%d" % e, tag="bank%d" % (5, 6, 1, 7)[e])
             nc.tensor.matmul_mx(
-                out=y_ps[e][:],
+                out=sums,
                 lhsT=w2_t[:, e, :].bitcast(FP4X4),
                 lhsT_scale=w_scales[:, E * H + N * e : E * H + N * (e + 1)],
-                rhs=h_codes[e][:].bitcast(FP8X4),
-                rhs_scale=h_scales[e][:],
+                rhs=h_codes[:, slots].bitcast(FP8X4),
+                rhs_scale=h_scales[:, slots],
                 start=True,
                 stop=True,
             )
 
-        def weigh(e):
-            nc.vector.tensor_tensor(y[:, C * e : C * (e + 1)], y_ps[e][:], gate_t[:, C * e : C * (e + 1)], MULT)
+        def weigh(e0, e1, sums):
+            nc.vector.tensor_tensor(y[:, C * e0 : C * e1], sums[:], gate_t[:, C * e0 : C * e1], MULT)
 
         def places(window, s0, s1):
             return window[:].indirect(dst_t[:, s0 // 16 : s1 // 16])
@@ -188,14 +189,15 @@ def tile_moe_two_mlp_gelu_kernel(tc, xT, w1_words, w1_scales, w2_words, w2_scale
         nc.sync.dma_start(out=w2_t[:].bitcast(I32), in_=w2_words[:, 0].rearrange("e p b -> p e b").bitcast(I32))
         nc.sync.dma_start(out=gate_t[:], in_=gate)
 
-        gather(1, second_row[0], 0, C)
-        gather(1, second_row[1], C, C)
-        permute(0, nc.scalar.copy)
+        gather(1, second_row[0], 0, 128)
+        gather(1, second_row[0], 128, 128)
         weave(0, nc.scalar.copy, U32, 0, 128)
+        permute(0, nc.scalar.copy)
         weave(0, nc.scalar.copy, U32, 128, C)
+        quant_x(0, 0, 128)
+        gather(1, second_row[1], C, C)
         weave(1, nc.scalar.copy, U32, 0, C)
         permute(1, nc.scalar.copy)
-        quant_x(0, 0, 128)
         quant_x(0, 128, C)
         layer1(0)
         gather(1, second_row[2], 2 * C, C)
@@ -211,17 +213,19 @@ def tile_moe_two_mlp_gelu_kernel(tc, xT, w1_words, w1_scales, w2_words, w2_scale
         quant_x(3, 0, C)
         layer1(3)
         y = keep.tile([P, S], F32, name="y", align_bytes=64, tag="x_codes3")
-        layer2(0)
-        layer2(1)
-        weigh(0)
-        layer2(2)
-        weigh(1)
-        weigh(2)
-        layer2(3)
+        sums_01 = psum.tile([P, 2 * C], F32, name="sums_01", tag="bank5")
+        sums_2 = psum.tile([P, C], F32, name="sums_2", tag="bank2")
+        sums_3 = psum.tile([P, C], F32, name="sums_3", tag="bank6")
+        layer2(0, sums_01[:, :C])
+        layer2(1, sums_01[:, C:])
+        layer2(2, sums_2[:])
+        weigh(0, 2, sums_01)
         cut = CUTS
-        nc.scalar.activation(places(placed_s, cut[0], cut[1]), y[:, cut[0] : cut[1]], COPY)
-        nc.vector.tensor_copy(places(placed_v, cut[1], cut[2]), y[:, cut[1] : cut[2]])
-        weigh(3)
+        nc.vector.tensor_copy(places(placed_v, cut[0], cut[1]), y[:, cut[0] : cut[1]])
+        layer2(3, sums_3[:])
+        nc.scalar.activation(places(placed_s, cut[1], cut[2]), y[:, cut[1] : cut[2]], COPY)
+        weigh(2, 3, sums_2)
+        weigh(3, 4, sums_3)
         nc.scalar.activation(places(placed_s, cut[2], cut[3]), y[:, cut[2] : cut[3]], COPY)
         nc.vector.tensor_copy(places(placed_v, cut[3], cut[4]), y[:, cut[3] : cut[4]])
         for k, (a, b) in enumerate(STORES):

@@ -20,16 +20,20 @@ K, T, E, C, H, N = 512, 1536, 4, 256, 512, 128
 S = E * C
 FLOPS = 2 * S * (K * H + H * N)
 
-X_LOADS = [[(0, 768, 768), (768, 768, 288)], [(0, 512, 512), (512, 832, 448), (1344, 192, 0)]]
-CUTS = (0, 192, 512, 768, S)
-STORES = [(a, a + 512) for a in range(0, T, 512)]
+BLOCK = 128
+LAYER1_BANKS = 5
+
+X_LOADS = [[(0, 768, 768), (768, 768, 288)], [(0, 768, 768), (768, 768, 256)]]
+
+VECTOR_FIRST, SCALAR_FIRST, SCALAR_SECOND, VECTOR_SECOND = (0, 192), (192, 2 * C), (2 * C, 3 * C), (3 * C, S)
+
+STORE_WIDTH = T // 3
 
 
 def tile_moe_two_mlp_gelu_kernel(tc, xT, w1_words, w1_scales, w2_words, w2_scales, gate, offs, dst, out):
     nc = tc.nc
     with ExitStack() as ctx:
         keep = ctx.enter_context(tc.tile_pool(name="keep", bufs=1))
-        late = ctx.enter_context(tc.tile_pool(name="late", bufs=1))
         psum = ctx.enter_context(tc.psum_pool(name="psum", bufs=1))
 
         offs_t = keep.tile([P, S // 16], U16, name="offs_t")
@@ -46,18 +50,13 @@ def tile_moe_two_mlp_gelu_kernel(tc, xT, w1_words, w1_scales, w2_words, w2_scale
         nc.gpsimd.memset(w_scales[:, E * H :].bitcast(I32), 0)
         nc.gpsimd.memset(placed_v[:], 0.0)
 
-        x_rows = xT.rearrange("(p h j) t -> h p j t", h=2, j=2)
-        x_raw = {}
+        x_rows = xT.rearrange("(p half j) t -> half p j t", half=2, j=2)
+        x_raw, w1_raw = {}, {}
 
-        def load_x(h, c):
-            t0, n = X_LOADS[h][c][:2]
-            if (h, c) == (1, len(X_LOADS[1]) - 1):
-                x_raw[h, c] = late.tile([P, 2, n], F32, name="x_raw%d_%d" % (h, c), align_bytes=64, offset=0)
-            else:
-                x_raw[h, c] = keep.tile([P, 2, n], F32, name="x_raw%d_%d" % (h, c))
-            nc.sync.dma_start(out=x_raw[h, c][:], in_=x_rows[h, :, :, t0 : t0 + n])
-
-        w1_raw = {}
+        def load_x(half, c):
+            t0, n = X_LOADS[half][c][:2]
+            x_raw[half, c] = keep.tile([P, 2, n], F32, name="x_raw%d_%d" % (half, c))
+            nc.sync.dma_start(out=x_raw[half, c][:], in_=x_rows[half, :, :, t0 : t0 + n])
 
         def load_w1(e0, e1):
             raw = keep.tile([P, (e1 - e0) * 2 * H], U8, name="w1_raw%d" % e0, align_bytes=64)
@@ -73,63 +72,66 @@ def tile_moe_two_mlp_gelu_kernel(tc, xT, w1_words, w1_scales, w2_words, w2_scale
             out=s1_raw[0:P:8, :].rearrange("q (e i) -> q e i", e=E).bitcast(I32),
             in_=w1_scales[:, 0].rearrange("e q i -> q e i").bitcast(I32),
         )
-        for c in range(1, len(X_LOADS[0])):
-            load_x(0, c)
+        load_x(0, 1)
         nc.sync.dma_start(offs_t[:], offs)
         nc.sync.dma_start(
-            out=w_scales[0:P:8, E * H :].rearrange("q (e i) -> q e i", e=E).bitcast(I32),
-            in_=w2_scales[:, 0].rearrange("e q i -> q e i").bitcast(I32),
+            out=w_scales[0:P:8, E * H :].rearrange("q (e n) -> q e n", e=E).bitcast(I32),
+            in_=w2_scales[:, 0].rearrange("e q n -> q e n").bitcast(I32),
         )
         for c in range(len(X_LOADS[1])):
             load_x(1, c)
         nc.vector.tensor_copy(
-            out=w_scales[:, : E * H].rearrange("p (e j c) -> p e j c", e=E, j=4),
-            in_=s1_raw[:].rearrange("p (e c j) -> p e j c", e=E, j=4),
+            out=w_scales[:, : E * H].rearrange("p (e j m) -> p e j m", e=E, j=4),
+            in_=s1_raw[:].rearrange("p (e m j) -> p e j m", e=E, j=4),
         )
         load_w1(0, 1)
-        load_w1(1, E)
+        load_w1(1, 2)
+        load_w1(2, E)
         for r in range(1, 4):
             nc.sync.dma_start(out=w_scales[r:P:32, :].bitcast(I32), in_=w_scales[8 * r : P : 32, :].bitcast(I32))
         nc.sync.dma_start(dst_t[:], dst)
 
-        pairs = [keep.tile([P, T, 2], BF16, name="pairs%d" % h, align_bytes=64) for h in range(2)]
+        pairs = [keep.tile([P, T, 2], BF16, name="pairs%d" % half, align_bytes=64) for half in range(2)]
         picked = keep.tile([P, 6, C], U32, name="picked", align_bytes=64)
-        first_row = [2, 3, 0, 1]
-        second_row = [4, 5, 2, 3]
+        picked_row = [[2, 3, 0, 1], [4, 5, 2, 3]]
 
-        def round_x(h):
-            for c, (t0, n, share) in enumerate(X_LOADS[h]):
+        def round_x(half):
+            for c, (t0, n, share) in enumerate(X_LOADS[half]):
                 for engine_copy, a, b in ((nc.scalar.copy, 0, share), (nc.vector.tensor_copy, share, n)):
                     if a < b:
                         engine_copy(
-                            out=pairs[h][:, t0 + a : t0 + b, :],
-                            in_=x_raw[h, c][:, :, a:b].rearrange("p j t -> p t j"),
+                            out=pairs[half][:, t0 + a : t0 + b, :],
+                            in_=x_raw[half, c][:, :, a:b].rearrange("p j t -> p t j"),
                         )
 
-        def gather(h, row, s0, n):
+        def gather(half, s0, n):
+            at = picked_row[half][s0 // C] * C + s0 % C
+            words = pairs[half][:].rearrange("p t j -> p (t j)").bitcast(U32)
             nc.vector.tensor_copy(
-                out=picked[:].rearrange("p r s -> p (r s)")[:, row * C + s0 % C : row * C + s0 % C + n],
-                in_=pairs[h][:].rearrange("p t j -> p (t j)").bitcast(U32).indirect(offs_t[:, s0 // 16 : (s0 + n) // 16]),
+                out=picked[:].rearrange("p r s -> p (r s)")[:, at : at + n],
+                in_=words.indirect(offs_t[:, s0 // 16 : (s0 + n) // 16]),
             )
 
-        grouped, w1_perm, x_codes, x_scales = {}, {}, {}, {}
+        woven, w1_perm, x_codes, x_scales = {}, {}, {}, {}
         h_raw = keep.tile([P, S, 4], BF16, name="h_raw", align_bytes=64)
         h_codes = keep.tile([P, S], U32, name="h_codes", align_bytes=64)
         h_scales = keep.tile([P, S], U8, name="h_scales", align_bytes=64)
 
-        def weave(e, engine_copy, dtype, a, b):
-            if e not in grouped:
-                grouped[e] = keep.tile([P, C, 4], BF16, name="grouped%d" % e, align_bytes=64, tag="grouped%d" % e)
-            r0, r1 = first_row[e], second_row[e]
-            words = grouped[e][:].rearrange("p s j -> p (s j)").bitcast(dtype).rearrange("p (s h) -> p s h", h=2)
-            both = picked[:].bitcast(dtype)[:, r0 : r1 + 1 : r1 - r0, a:b]
-            engine_copy(out=words[:, a:b, :], in_=both.rearrange("p h s -> p s h"))
+        def weave(e, engine_copy, word, a, b):
+            if e not in woven:
+                woven[e] = keep.tile([P, C, 4], BF16, name="woven%d" % e, align_bytes=64, tag="woven%d" % e)
+            r0, r1 = picked_row[0][e], picked_row[1][e]
+            target = woven[e][:].rearrange("p s d -> p (s d)").bitcast(word).rearrange("p (s half) -> p s half", half=2)
+            both = picked[:].bitcast(word)[:, r0 : r1 + 1 : r1 - r0, a:b]
+            engine_copy(out=target[:, a:b, :], in_=both.rearrange("p half s -> p s half"))
+
+        perm_tag = ("w1_perm0", "w1_perm1", "woven0", "woven2")
 
         def permute(e, engine_copy):
-            w1_perm[e] = keep.tile([P, 2 * H], U8, name="w1_perm%d" % e, align_bytes=64, tag=("w1_perm0", "w1_perm1", "grouped0", "grouped2")[e])
+            w1_perm[e] = keep.tile([P, 2 * H], U8, name="w1_perm%d" % e, align_bytes=64, tag=perm_tag[e])
             engine_copy(
-                out=w1_perm[e][:].bitcast(U16).rearrange("p (j c) -> p j c", j=4),
-                in_=w1_raw[e].bitcast(U16).rearrange("p (c j) -> p j c", j=4),
+                out=w1_perm[e][:].bitcast(U16).rearrange("p (j m) -> p j m", j=4),
+                in_=w1_raw[e].bitcast(U16).rearrange("p (m j) -> p j m", j=4),
             )
 
         def quant_x(e, a, b):
@@ -139,23 +141,27 @@ def tile_moe_two_mlp_gelu_kernel(tc, xT, w1_words, w1_scales, w2_words, w2_scale
             nc.vector.quantize_mx(
                 out=x_codes[e][:, a:b].bitcast(FP8X4),
                 scales=x_scales[e][:, a:b],
-                in_=grouped[e][:, a:b, :].rearrange("p s j -> p (s j)"),
+                in_=woven[e][:, a:b, :].rearrange("p s d -> p (s d)"),
             )
 
+        def block_bank(s0):
+            return "bank%d" % (s0 // BLOCK % LAYER1_BANKS)
+
         def layer1(e):
-            for a in (0, 128):
-                acc = psum.tile([P, 4, 128], F32, name="acc", tag="bank%d" % ((2 * e + a // 128) % 5))
+            for a in range(0, C, BLOCK):
+                s0 = C * e + a
+                acc = psum.tile([P, 4, BLOCK], F32, name="acc", tag=block_bank(s0))
                 for j in range(4):
                     nc.tensor.matmul_mx(
                         out=acc[:, j, :],
-                        lhsT=w1_perm[e][:, 256 * j : 256 * (j + 1)].bitcast(FP4X4),
-                        lhsT_scale=w_scales[:, H * e + 128 * j : H * e + 128 * (j + 1)],
-                        rhs=x_codes[e][:, a : a + 128].bitcast(FP8X4),
-                        rhs_scale=x_scales[e][:, a : a + 128],
+                        lhsT=w1_perm[e][:, 2 * P * j : 2 * P * (j + 1)].bitcast(FP4X4),
+                        lhsT_scale=w_scales[:, H * e + P * j : H * e + P * (j + 1)],
+                        rhs=x_codes[e][:, a : a + BLOCK].bitcast(FP8X4),
+                        rhs_scale=x_scales[e][:, a : a + BLOCK],
                         start=True,
                         stop=True,
                     )
-                nc.scalar.activation(out=h_raw[:, C * e + a : C * e + a + 128, :], in_=acc[:].rearrange("p j s -> p s j"), func=GELU)
+                nc.scalar.activation(out=h_raw[:, s0 : s0 + BLOCK, :], in_=acc[:].rearrange("p j s -> p s j"), func=GELU)
 
         def layer2(e, sums):
             slots = slice(C * e, C * (e + 1))
@@ -177,58 +183,62 @@ def tile_moe_two_mlp_gelu_kernel(tc, xT, w1_words, w1_scales, w2_words, w2_scale
         def weigh(e0, e1, sums):
             nc.vector.tensor_tensor(y[:, C * e0 : C * e1], sums[:], gate_t[:, C * e0 : C * e1], MULT)
 
-        def places(window, s0, s1):
-            return window[:].indirect(dst_t[:, s0 // 16 : s1 // 16])
+        def scatter_vector(s0, s1):
+            nc.vector.tensor_copy(placed_v[:].indirect(dst_t[:, s0 // 16 : s1 // 16]), y[:, s0:s1])
+
+        def scatter_scalar(s0, s1):
+            nc.scalar.activation(placed_s[:].indirect(dst_t[:, s0 // 16 : s1 // 16]), y[:, s0:s1], COPY)
 
         round_x(0)
-        gather(0, first_row[0], 0, 2 * C)
-        gather(0, first_row[2], 2 * C, 2 * C)
+        gather(0, 0, 2 * C)
+        gather(0, 2 * C, 2 * C)
         round_x(1)
-        w2_t = late.tile([P, E, 2 * N], U8, name="w2_t", align_bytes=64, offset=0)
-        gate_t = late.tile([P, S], F32, name="gate_t", align_bytes=64, offset=E * 2 * N)
+        w2_t = keep.tile([P, E, 2 * N], U8, name="w2_t", align_bytes=64)
+        gate_t = keep.tile([P, S], F32, name="gate_t", align_bytes=64)
         nc.sync.dma_start(out=w2_t[:].bitcast(I32), in_=w2_words[:, 0].rearrange("e p b -> p e b").bitcast(I32))
         nc.sync.dma_start(out=gate_t[:], in_=gate)
 
-        gather(1, second_row[0], 0, 128)
-        gather(1, second_row[0], 128, 128)
-        weave(0, nc.scalar.copy, U32, 0, 128)
+        gather(1, 0, BLOCK)
+        gather(1, BLOCK, BLOCK)
+        weave(0, nc.scalar.copy, U32, 0, BLOCK)
         permute(0, nc.scalar.copy)
-        weave(0, nc.scalar.copy, U32, 128, C)
-        quant_x(0, 0, 128)
-        gather(1, second_row[1], C, C)
+        weave(0, nc.scalar.copy, U32, BLOCK, C)
+        quant_x(0, 0, BLOCK)
+        gather(1, C, C)
         weave(1, nc.scalar.copy, U32, 0, C)
         permute(1, nc.scalar.copy)
-        quant_x(0, 128, C)
+        quant_x(0, BLOCK, C)
         layer1(0)
-        gather(1, second_row[2], 2 * C, C)
+        gather(1, 2 * C, C)
         permute(2, nc.vector.tensor_copy)
         quant_x(1, 0, C)
         layer1(1)
         weave(2, nc.vector.tensor_copy, I32, 0, C)
-        gather(1, second_row[3], 3 * C, C)
+        gather(1, 3 * C, C)
         quant_x(2, 0, C)
         layer1(2)
         weave(3, nc.vector.tensor_copy, I32, 0, C)
         permute(3, nc.vector.tensor_copy)
         quant_x(3, 0, C)
         layer1(3)
+
         y = keep.tile([P, S], F32, name="y", align_bytes=64, tag="x_codes3")
-        sums_01 = psum.tile([P, 2 * C], F32, name="sums_01", tag="bank5")
-        sums_2 = psum.tile([P, C], F32, name="sums_2", tag="bank2")
-        sums_3 = psum.tile([P, C], F32, name="sums_3", tag="bank6")
+        sums_01 = psum.tile([P, 2 * C], F32, name="sums_01", tag="bank%d" % LAYER1_BANKS)
+        sums_2 = psum.tile([P, C], F32, name="sums_2", tag=block_bank(S - BLOCK))
+        sums_3 = psum.tile([P, C], F32, name="sums_3", tag="bank%d" % (LAYER1_BANKS + 1))
         layer2(0, sums_01[:, :C])
         layer2(1, sums_01[:, C:])
         layer2(2, sums_2[:])
         weigh(0, 2, sums_01)
-        cut = CUTS
-        nc.vector.tensor_copy(places(placed_v, cut[0], cut[1]), y[:, cut[0] : cut[1]])
+        scatter_vector(*VECTOR_FIRST)
         layer2(3, sums_3[:])
-        nc.scalar.activation(places(placed_s, cut[1], cut[2]), y[:, cut[1] : cut[2]], COPY)
+        scatter_scalar(*SCALAR_FIRST)
         weigh(2, 3, sums_2)
         weigh(3, 4, sums_3)
-        nc.scalar.activation(places(placed_s, cut[2], cut[3]), y[:, cut[2] : cut[3]], COPY)
-        nc.vector.tensor_copy(places(placed_v, cut[3], cut[4]), y[:, cut[3] : cut[4]])
-        for k, (a, b) in enumerate(STORES):
-            nc.vector.tensor_tensor(placed_v[:, a:b], placed_v[:, a:b], placed_s[:, a:b], ADD)
-            queue = nc.sync if k % 2 == 0 else nc.scalar
-            queue.dma_start(out=out[:, a:b], in_=placed_v[:, a:b])
+        scatter_scalar(*SCALAR_SECOND)
+        scatter_vector(*VECTOR_SECOND)
+
+        for a, queue in zip(range(0, T, STORE_WIDTH), (nc.sync, nc.scalar, nc.sync)):
+            piece = slice(a, a + STORE_WIDTH)
+            nc.vector.tensor_tensor(placed_v[:, piece], placed_v[:, piece], placed_s[:, piece], ADD)
+            queue.dma_start(out=out[:, piece], in_=placed_v[:, piece])

@@ -25,7 +25,7 @@ LAYER1_BANKS = 5
 
 X_LOADS = [[(0, 768, 768), (768, 768, 288)], [(0, 768, 768), (768, 768, 256)]]
 
-VECTOR_FIRST, SCALAR_FIRST, SCALAR_SECOND, VECTOR_SECOND = (0, 192), (192, 2 * C), (2 * C, 3 * C), (3 * C, S)
+VECTOR_FIRST, SCALAR_FIRST, SCALAR_SECOND, VECTOR_SECOND = (0, 160), (160, 2 * C), (2 * C, 3 * C), (3 * C, S)
 
 STORE_WIDTH = T // 3
 
@@ -49,6 +49,8 @@ def tile_moe_two_mlp_gelu_kernel(tc, xT, w1_words, w1_scales, w2_words, w2_scale
         nc.scalar.activation(out=placed_s[:], in_=zero[:].to_broadcast([P, T]), func=GELU)
         nc.gpsimd.memset(w_scales[:, E * H :].bitcast(I32), 0)
         nc.gpsimd.memset(placed_v[:], 0.0)
+        zeros = keep.tile([P, VECTOR_FIRST[1]], F32, name="zeros")
+        nc.gpsimd.memset(zeros[:], 0.0)
 
         x_rows = xT.rearrange("(p half j) t -> half p j t", half=2, j=2)
         x_raw, w1_raw = {}, {}
@@ -93,7 +95,7 @@ def tile_moe_two_mlp_gelu_kernel(tc, xT, w1_words, w1_scales, w2_words, w2_scale
 
         pairs = [keep.tile([P, T, 2], BF16, name="pairs%d" % half, align_bytes=64) for half in range(2)]
         picked = keep.tile([P, 6, C], U32, name="picked", align_bytes=64)
-        picked_row = [[2, 3, 0, 1], [4, 5, 2, 3]]
+        picked_row = [[0, 1, 2, 3], [4, 5, 0, 1]]
 
         def round_x(half):
             for c, (t0, n, share) in enumerate(X_LOADS[half]):
@@ -122,7 +124,7 @@ def tile_moe_two_mlp_gelu_kernel(tc, xT, w1_words, w1_scales, w2_words, w2_scale
                 woven[e] = keep.tile([P, C, 4], BF16, name="woven%d" % e, align_bytes=64, tag="woven%d" % e)
             r0, r1 = picked_row[0][e], picked_row[1][e]
             target = woven[e][:].rearrange("p s d -> p (s d)").bitcast(word).rearrange("p (s half) -> p s half", half=2)
-            both = picked[:].bitcast(word)[:, r0 : r1 + 1 : r1 - r0, a:b]
+            both = picked[:].bitcast(word)[:, r0 :: r1 - r0, a:b][:, :2, :]
             engine_copy(out=target[:, a:b, :], in_=both.rearrange("p half s -> p s half"))
 
         perm_tag = ("w1_perm0", "w1_perm1", "woven0", "woven2")
@@ -190,8 +192,7 @@ def tile_moe_two_mlp_gelu_kernel(tc, xT, w1_words, w1_scales, w2_words, w2_scale
             nc.scalar.activation(placed_s[:].indirect(dst_t[:, s0 // 16 : s1 // 16]), y[:, s0:s1], COPY)
 
         round_x(0)
-        gather(0, 0, 2 * C)
-        gather(0, 2 * C, 2 * C)
+        gather(0, 0, S)
         round_x(1)
         w2_t = keep.tile([P, E, 2 * N], U8, name="w2_t", align_bytes=64)
         gate_t = keep.tile([P, S], F32, name="gate_t", align_bytes=64)
@@ -230,7 +231,8 @@ def tile_moe_two_mlp_gelu_kernel(tc, xT, w1_words, w1_scales, w2_words, w2_scale
         layer2(1, sums_01[:, C:])
         layer2(2, sums_2[:])
         weigh(0, 2, sums_01)
-        scatter_vector(*VECTOR_FIRST)
+        s0, s1 = VECTOR_FIRST
+        nc.vector.tensor_tensor(placed_v[:].indirect(dst_t[:, s0 // 16 : s1 // 16]), y[:, s0:s1], zeros[:], ADD)
         layer2(3, sums_3[:])
         scatter_scalar(*SCALAR_FIRST)
         weigh(2, 3, sums_2)

@@ -25,7 +25,7 @@ LAYER1_BANKS = 5
 
 X_LOADS = [[(0, 768, 768), (768, 768, 288)], [(0, 768, 768), (768, 768, 256)]]
 
-VECTOR_FIRST, SCALAR_FIRST, SCALAR_SECOND, VECTOR_SECOND = (0, 160), (160, 2 * C), (2 * C, 3 * C), (3 * C, S)
+VECTOR_FIRST, SCALAR_FIRST, SCALAR_SECOND, VECTOR_SECOND = (0, 128), (128, 2 * C), (2 * C, 3 * C), (3 * C, S)
 
 STORE_WIDTH = T // 3
 

@@ -23,7 +23,7 @@ FLOPS = 2 * S * (K * H + H * N)
 BLOCK = 128
 LAYER1_BANKS = 5
 
-X_LOADS = [[(0, 768, 768), (768, 768, 288)], [(0, 768, 768), (768, 768, 256)]]
+X_LOADS = [[(0, 768, 768), (768, 768, 240)], [(0, 768, 672), (768, 768, 240)]]
 
 VECTOR_FIRST, SCALAR_FIRST, SCALAR_SECOND, VECTOR_SECOND = (0, 128), (128, 2 * C), (2 * C, 3 * C), (3 * C, S)
 

@@ -57,7 +57,7 @@ def tile_moe_two_mlp_gelu_kernel(tc, xT, w1_words, w1_scales, w2_words, w2_scale
 
         def load_x(half, c):
             t0, n = X_LOADS[half][c][:2]
-            x_raw[half, c] = keep.tile([P, 2, n], F32, name="x_raw%d_%d" % (half, c))
+            x_raw[half, c] = keep.tile([P, 2, n], F32, name="x_raw%d_%d" % (half, c), align_bytes=64, tag="x_raw%d_%d" % (half, c))
             nc.sync.dma_start(out=x_raw[half, c][:], in_=x_rows[half, :, :, t0 : t0 + n])
 
         def load_w1(e0, e1):
@@ -86,9 +86,8 @@ def tile_moe_two_mlp_gelu_kernel(tc, xT, w1_words, w1_scales, w2_words, w2_scale
             out=w_scales[:, : E * H].rearrange("p (e j m) -> p e j m", e=E, j=4),
             in_=s1_raw[:].rearrange("p (e m j) -> p e j m", e=E, j=4),
         )
-        load_w1(0, 1)
-        load_w1(1, 2)
-        load_w1(2, E)
+        for e in (0, 2, 1, 3):
+            load_w1(e, e + 1)
         for r in range(1, 4):
             nc.sync.dma_start(out=w_scales[r:P:32, :].bitcast(I32), in_=w_scales[8 * r : P : 32, :].bitcast(I32))
         nc.sync.dma_start(dst_t[:], dst)
@@ -127,7 +126,7 @@ def tile_moe_two_mlp_gelu_kernel(tc, xT, w1_words, w1_scales, w2_words, w2_scale
             both = picked[:].bitcast(word)[:, r0 :: r1 - r0, a:b][:, :2, :]
             engine_copy(out=target[:, a:b, :], in_=both.rearrange("p half s -> p s half"))
 
-        perm_tag = ("w1_perm0", "w1_perm1", "woven0", "woven2")
+        perm_tag = ("w1_perm0", "w1_perm1", "x_raw1_0", "woven2")
 
         def permute(e, engine_copy):
             w1_perm[e] = keep.tile([P, 2 * H], U8, name="w1_perm%d" % e, align_bytes=64, tag=perm_tag[e])
@@ -194,6 +193,7 @@ def tile_moe_two_mlp_gelu_kernel(tc, xT, w1_words, w1_scales, w2_words, w2_scale
         round_x(0)
         gather(0, 0, S)
         round_x(1)
+        permute(2, nc.vector.tensor_copy)
         w2_t = keep.tile([P, E, 2 * N], U8, name="w2_t", align_bytes=64)
         gate_t = keep.tile([P, S], F32, name="gate_t", align_bytes=64)
         nc.sync.dma_start(out=w2_t[:].bitcast(I32), in_=w2_words[:, 0].rearrange("e p b -> p e b").bitcast(I32))
@@ -211,7 +211,6 @@ def tile_moe_two_mlp_gelu_kernel(tc, xT, w1_words, w1_scales, w2_words, w2_scale
         quant_x(0, BLOCK, C)
         layer1(0)
         gather(1, 2 * C, C)
-        permute(2, nc.vector.tensor_copy)
         quant_x(1, 0, C)
         layer1(1)
         weave(2, nc.vector.tensor_copy, I32, 0, C)

@@ -21,12 +21,9 @@ S = E * C
 FLOPS = 2 * S * (K * H + H * N)
 
 BLOCK = 128
-LAYER1_BANKS = 5
-
-X_LOADS = [[(0, 768, 768), (768, 768, 240)], [(0, 768, 672), (768, 768, 240)]]
-
-VECTOR_FIRST, SCALAR_FIRST, SCALAR_SECOND, VECTOR_SECOND = (0, 128), (128, 2 * C), (2 * C, 3 * C), (3 * C, S)
-
+LAYER1_BANKS = 3
+SPLITS = (480, 480, 704, 704)
+VECTOR_FIRST, SCALAR_FIRST, SCALAR_SECOND, VECTOR_SECOND = (0, 160), (160, 2 * C), (2 * C, 3 * C), (3 * C, S)
 STORE_WIDTH = T // 3
 
 
@@ -52,97 +49,75 @@ def tile_moe_two_mlp_gelu_kernel(tc, xT, w1_words, w1_scales, w2_words, w2_scale
         zeros = keep.tile([P, VECTOR_FIRST[1]], F32, name="zeros")
         nc.gpsimd.memset(zeros[:], 0.0)
 
-        x_rows = xT.rearrange("(p half j) t -> half p j t", half=2, j=2)
-        x_raw, w1_raw = {}, {}
-
-        def load_x(half, c):
-            t0, n = X_LOADS[half][c][:2]
-            x_raw[half, c] = keep.tile([P, 2, n], F32, name="x_raw%d_%d" % (half, c), align_bytes=64, tag="x_raw%d_%d" % (half, c))
-            nc.sync.dma_start(out=x_raw[half, c][:], in_=x_rows[half, :, :, t0 : t0 + n])
+        w1_raw = {}
 
         def load_w1(e0, e1):
-            raw = keep.tile([P, (e1 - e0) * 2 * H], U8, name="w1_raw%d" % e0, align_bytes=64)
-            nc.sync.dma_start(
-                out=raw[:].rearrange("p (e b) -> p e b", b=2 * H).bitcast(I32),
-                in_=w1_words[e0:e1, 0].rearrange("e p b -> p e b").bitcast(I32),
-            )
+            raw = keep.tile([P, e1 - e0, 2 * H], U8, name="w1_raw%d" % e0, align_bytes=256)
+            nc.sync.dma_start(out=raw[:].bitcast(I32), in_=w1_words[e0:e1, 0].rearrange("e p b -> p e b").bitcast(I32))
             for e in range(e0, e1):
-                w1_raw[e] = raw[:, 2 * H * (e - e0) : 2 * H * (e - e0 + 1)]
+                w1_raw[e] = raw[:, e - e0, :]
 
-        load_x(0, 0)
+        load_w1(0, 2)
         nc.sync.dma_start(
             out=s1_raw[0:P:8, :].rearrange("q (e i) -> q e i", e=E).bitcast(I32),
             in_=w1_scales[:, 0].rearrange("e q i -> q e i").bitcast(I32),
         )
-        load_x(0, 1)
+        x_rows = xT.rearrange("(p d) t -> d p t", d=4)
+        planes = [keep.tile([P, T], F32, name="plane%d" % d, align_bytes=256) for d in range(4)]
+        nc.sync.dma_start(out=planes[2][:], in_=x_rows[2])
         nc.sync.dma_start(offs_t[:], offs)
         nc.sync.dma_start(
             out=w_scales[0:P:8, E * H :].rearrange("q (e n) -> q e n", e=E).bitcast(I32),
             in_=w2_scales[:, 0].rearrange("e q n -> q e n").bitcast(I32),
         )
-        for c in range(len(X_LOADS[1])):
-            load_x(1, c)
+        for d in (0, 1, 3):
+            nc.sync.dma_start(out=planes[d][:], in_=x_rows[d])
         nc.vector.tensor_copy(
             out=w_scales[:, : E * H].rearrange("p (e j m) -> p e j m", e=E, j=4),
             in_=s1_raw[:].rearrange("p (e m j) -> p e j m", e=E, j=4),
         )
-        for e in (0, 2, 1, 3):
-            load_w1(e, e + 1)
+        load_w1(2, 4)
         for r in range(1, 4):
             nc.sync.dma_start(out=w_scales[r:P:32, :].bitcast(I32), in_=w_scales[8 * r : P : 32, :].bitcast(I32))
+        w2_t = keep.tile([P, E, 2 * N], U8, name="w2_t", align_bytes=64)
+        gate_t = keep.tile([P, S], F32, name="gate_t", align_bytes=64)
+        nc.sync.dma_start(out=w2_t[:].bitcast(I32), in_=w2_words[:, 0].rearrange("e p b -> p e b").bitcast(I32))
         nc.sync.dma_start(dst_t[:], dst)
+        nc.sync.dma_start(out=gate_t[:], in_=gate)
 
-        pairs = [keep.tile([P, T, 2], BF16, name="pairs%d" % half, align_bytes=64) for half in range(2)]
-        picked = keep.tile([P, 6, C], U32, name="picked", align_bytes=64)
-        picked_row = [[0, 1, 2, 3], [4, 5, 0, 1]]
+        w1_perm = keep.tile([P, E, 2 * H], U8, name="w1_perm", align_bytes=64)
 
-        def round_x(half):
-            for c, (t0, n, share) in enumerate(X_LOADS[half]):
-                for engine_copy, a, b in ((nc.scalar.copy, 0, share), (nc.vector.tensor_copy, share, n)):
-                    if a < b:
-                        engine_copy(
-                            out=pairs[half][:, t0 + a : t0 + b, :],
-                            in_=x_raw[half, c][:, :, a:b].rearrange("p j t -> p t j"),
-                        )
-
-        def gather(half, s0, n):
-            at = picked_row[half][s0 // C] * C + s0 % C
-            words = pairs[half][:].rearrange("p t j -> p (t j)").bitcast(U32)
-            nc.vector.tensor_copy(
-                out=picked[:].rearrange("p r s -> p (r s)")[:, at : at + n],
-                in_=words.indirect(offs_t[:, s0 // 16 : (s0 + n) // 16]),
+        def permute(e, engine_copy):
+            engine_copy(
+                out=w1_perm[:, e, :].bitcast(U16).rearrange("p (j m) -> p j m", j=4),
+                in_=w1_raw[e].bitcast(U16).rearrange("p (m j) -> p j m", j=4),
             )
 
-        woven, w1_perm, x_codes, x_scales = {}, {}, {}, {}
+        permute(0, nc.scalar.copy)
+        permute(1, nc.scalar.copy)
+
+        woven = keep.tile([P, S, 4], BF16, name="woven", align_bytes=64)
+
+        def picked(d, s0, s1):
+            return planes[d][:].indirect(offs_t[:, s0 // 16 : s1 // 16])
+
+        def gather_vector(d, s0, s1):
+            nc.vector.tensor_copy(out=woven[:, s0:s1, d], in_=picked(d, s0, s1))
+
+        def gather_scalar(d, s0, s1):
+            nc.scalar.activation(out=woven[:, s0:s1, d], in_=picked(d, s0, s1), func=COPY)
+
+        x_codes = keep.tile([P, S], U32, name="x_codes", align_bytes=64)
+        x_scales = keep.tile([P, S], U8, name="x_scales", align_bytes=64)
         h_raw = keep.tile([P, S, 4], BF16, name="h_raw", align_bytes=64)
         h_codes = keep.tile([P, S], U32, name="h_codes", align_bytes=64)
         h_scales = keep.tile([P, S], U8, name="h_scales", align_bytes=64)
 
-        def weave(e, engine_copy, word, a, b):
-            if e not in woven:
-                woven[e] = keep.tile([P, C, 4], BF16, name="woven%d" % e, align_bytes=64, tag="woven%d" % e)
-            r0, r1 = picked_row[0][e], picked_row[1][e]
-            target = woven[e][:].rearrange("p s d -> p (s d)").bitcast(word).rearrange("p (s half) -> p s half", half=2)
-            both = picked[:].bitcast(word)[:, r0 :: r1 - r0, a:b][:, :2, :]
-            engine_copy(out=target[:, a:b, :], in_=both.rearrange("p half s -> p s half"))
-
-        perm_tag = ("w1_perm0", "w1_perm1", "x_raw1_0", "woven2")
-
-        def permute(e, engine_copy):
-            w1_perm[e] = keep.tile([P, 2 * H], U8, name="w1_perm%d" % e, align_bytes=64, tag=perm_tag[e])
-            engine_copy(
-                out=w1_perm[e][:].bitcast(U16).rearrange("p (j m) -> p j m", j=4),
-                in_=w1_raw[e].bitcast(U16).rearrange("p (m j) -> p j m", j=4),
-            )
-
-        def quant_x(e, a, b):
-            if e not in x_codes:
-                x_codes[e] = keep.tile([P, C], U32, name="x_codes%d" % e, align_bytes=64, tag="x_codes%d" % e)
-                x_scales[e] = keep.tile([P, C], U8, name="x_scales%d" % e, align_bytes=64)
+        def quant_x(s0, s1):
             nc.vector.quantize_mx(
-                out=x_codes[e][:, a:b].bitcast(FP8X4),
-                scales=x_scales[e][:, a:b],
-                in_=woven[e][:, a:b, :].rearrange("p s d -> p (s d)"),
+                out=x_codes[:, s0:s1].bitcast(FP8X4),
+                scales=x_scales[:, s0:s1],
+                in_=woven[:, s0:s1, :].rearrange("p s d -> p (s d)"),
             )
 
         def block_bank(s0):
@@ -155,10 +130,10 @@ def tile_moe_two_mlp_gelu_kernel(tc, xT, w1_words, w1_scales, w2_words, w2_scale
                 for j in range(4):
                     nc.tensor.matmul_mx(
                         out=acc[:, j, :],
-                        lhsT=w1_perm[e][:, 2 * P * j : 2 * P * (j + 1)].bitcast(FP4X4),
+                        lhsT=w1_perm[:, e, 2 * P * j : 2 * P * (j + 1)].bitcast(FP4X4),
                         lhsT_scale=w_scales[:, H * e + P * j : H * e + P * (j + 1)],
-                        rhs=x_codes[e][:, a : a + BLOCK].bitcast(FP8X4),
-                        rhs_scale=x_scales[e][:, a : a + BLOCK],
+                        rhs=x_codes[:, s0 : s0 + BLOCK].bitcast(FP8X4),
+                        rhs_scale=x_scales[:, s0 : s0 + BLOCK],
                         start=True,
                         stop=True,
                     )
@@ -190,48 +165,35 @@ def tile_moe_two_mlp_gelu_kernel(tc, xT, w1_words, w1_scales, w2_words, w2_scale
         def scatter_scalar(s0, s1):
             nc.scalar.activation(placed_s[:].indirect(dst_t[:, s0 // 16 : s1 // 16]), y[:, s0:s1], COPY)
 
-        round_x(0)
-        gather(0, 0, S)
-        round_x(1)
+        for d in (2, 0, 1):
+            gather_scalar(d, 0, SPLITS[d])
+            gather_vector(d, SPLITS[d], S)
+        gather_vector(3, SPLITS[3], S)
+        gather_scalar(3, 0, BLOCK)
+        gather_scalar(3, BLOCK, 3 * BLOCK)
+        gather_scalar(3, 3 * BLOCK, SPLITS[3])
+        quant_x(0, BLOCK)
+        quant_x(BLOCK, 3 * BLOCK)
+        quant_x(3 * BLOCK, 3 * C)
         permute(2, nc.vector.tensor_copy)
-        w2_t = keep.tile([P, E, 2 * N], U8, name="w2_t", align_bytes=64)
-        gate_t = keep.tile([P, S], F32, name="gate_t", align_bytes=64)
-        nc.sync.dma_start(out=w2_t[:].bitcast(I32), in_=w2_words[:, 0].rearrange("e p b -> p e b").bitcast(I32))
-        nc.sync.dma_start(out=gate_t[:], in_=gate)
-
-        gather(1, 0, BLOCK)
-        gather(1, BLOCK, BLOCK)
-        weave(0, nc.scalar.copy, U32, 0, BLOCK)
-        permute(0, nc.scalar.copy)
-        weave(0, nc.scalar.copy, U32, BLOCK, C)
-        quant_x(0, 0, BLOCK)
-        gather(1, C, C)
-        weave(1, nc.scalar.copy, U32, 0, C)
-        permute(1, nc.scalar.copy)
-        quant_x(0, BLOCK, C)
-        layer1(0)
-        gather(1, 2 * C, C)
-        quant_x(1, 0, C)
-        layer1(1)
-        weave(2, nc.vector.tensor_copy, I32, 0, C)
-        gather(1, 3 * C, C)
-        quant_x(2, 0, C)
-        layer1(2)
-        weave(3, nc.vector.tensor_copy, I32, 0, C)
+        quant_x(3 * C, S)
         permute(3, nc.vector.tensor_copy)
-        quant_x(3, 0, C)
-        layer1(3)
-
-        y = keep.tile([P, S], F32, name="y", align_bytes=64, tag="x_codes3")
-        sums_01 = psum.tile([P, 2 * C], F32, name="sums_01", tag="bank%d" % LAYER1_BANKS)
-        sums_2 = psum.tile([P, C], F32, name="sums_2", tag=block_bank(S - BLOCK))
+        layer1(0)
+        layer1(1)
+        y = keep.tile([P, S], F32, name="y", align_bytes=64)
+        sums_0 = psum.tile([P, C], F32, name="sums_0", tag="bank%d" % LAYER1_BANKS)
+        sums_1 = psum.tile([P, C], F32, name="sums_1", tag="bank%d" % (LAYER1_BANKS + 2))
         sums_3 = psum.tile([P, C], F32, name="sums_3", tag="bank%d" % (LAYER1_BANKS + 1))
-        layer2(0, sums_01[:, :C])
-        layer2(1, sums_01[:, C:])
-        layer2(2, sums_2[:])
-        weigh(0, 2, sums_01)
+        layer2(0, sums_0[:])
+        weigh(0, 1, sums_0)
+        layer1(2)
+        layer2(1, sums_1[:])
+        layer1(3)
+        sums_2 = psum.tile([P, C], F32, name="sums_2", tag=block_bank(S - BLOCK))
         s0, s1 = VECTOR_FIRST
         nc.vector.tensor_tensor(placed_v[:].indirect(dst_t[:, s0 // 16 : s1 // 16]), y[:, s0:s1], zeros[:], ADD)
+        weigh(1, 2, sums_1)
+        layer2(2, sums_2[:])
         layer2(3, sums_3[:])
         scatter_scalar(*SCALAR_FIRST)
         weigh(2, 3, sums_2)

@@ -22,8 +22,8 @@ FLOPS = 2 * S * (K * H + H * N)
 
 BLOCK = 128
 LAYER1_BANKS = 3
-SPLITS = (480, 480, 704, 704)
-VECTOR_FIRST, SCALAR_FIRST, SCALAR_SECOND, VECTOR_SECOND = (0, 160), (160, 2 * C), (2 * C, 3 * C), (3 * C, S)
+SPLITS = (832, 832, 576, 576)
+VECTOR_FIRST, SCALAR_FIRST, SCALAR_SECOND, VECTOR_SECOND = (0, 128), (128, 2 * C), (2 * C, 3 * C), (3 * C, S)
 STORE_WIDTH = T // 3
 
 
@@ -96,16 +96,30 @@ def tile_moe_two_mlp_gelu_kernel(tc, xT, w1_words, w1_scales, w2_words, w2_scale
         permute(0, nc.scalar.copy)
         permute(1, nc.scalar.copy)
 
-        woven = keep.tile([P, S, 4], BF16, name="woven", align_bytes=64)
+        woven = {}
+        for block in range(C // BLOCK):
+            woven[BLOCK * block] = keep.tile([P, BLOCK, 4], BF16, name="first%d" % block, align_bytes=64, tag="first%d" % block)
+        pairs = keep.tile([P, 2, S - C, 2], BF16, name="pairs", align_bytes=64)
 
         def picked(d, s0, s1):
             return planes[d][:].indirect(offs_t[:, s0 // 16 : s1 // 16])
 
         def gather_vector(d, s0, s1):
-            nc.vector.tensor_copy(out=woven[:, s0:s1, d], in_=picked(d, s0, s1))
+            nc.vector.tensor_copy(out=pairs[:, d // 2, s0 - C : s1 - C, d % 2], in_=picked(d, s0, s1))
 
         def gather_scalar(d, s0, s1):
-            nc.scalar.activation(out=woven[:, s0:s1, d], in_=picked(d, s0, s1), func=COPY)
+            nc.scalar.activation(out=pairs[:, d // 2, s0 - C : s1 - C, d % 2], in_=picked(d, s0, s1), func=COPY)
+
+        def gather_first(d, s0):
+            nc.scalar.activation(out=woven[s0][:, :, d], in_=picked(d, s0, s0 + BLOCK), func=COPY)
+
+        def weave(e, tag):
+            woven[C * e] = keep.tile([P, C, 4], BF16, name="woven%d" % e, align_bytes=64, tag=tag)
+            words = pairs[:].rearrange("p half s j -> p half (s j)").bitcast(I32)
+            nc.vector.tensor_copy(
+                out=woven[C * e][:].rearrange("p s d -> p (s d)").bitcast(I32).rearrange("p (s half) -> p s half", half=2),
+                in_=words[:, :, C * (e - 1) : C * e].rearrange("p half s -> p s half"),
+            )
 
         x_codes = keep.tile([P, S], U32, name="x_codes", align_bytes=64)
         x_scales = keep.tile([P, S], U8, name="x_scales", align_bytes=64)
@@ -117,7 +131,7 @@ def tile_moe_two_mlp_gelu_kernel(tc, xT, w1_words, w1_scales, w2_words, w2_scale
             nc.vector.quantize_mx(
                 out=x_codes[:, s0:s1].bitcast(FP8X4),
                 scales=x_scales[:, s0:s1],
-                in_=woven[:, s0:s1, :].rearrange("p s d -> p (s d)"),
+                in_=woven[s0][:].rearrange("p s d -> p (s d)"),
             )
 
         def block_bank(s0):
@@ -165,19 +179,19 @@ def tile_moe_two_mlp_gelu_kernel(tc, xT, w1_words, w1_scales, w2_words, w2_scale
         def scatter_scalar(s0, s1):
             nc.scalar.activation(placed_s[:].indirect(dst_t[:, s0 // 16 : s1 // 16]), y[:, s0:s1], COPY)
 
-        for d in (2, 0, 1):
-            gather_scalar(d, 0, SPLITS[d])
-            gather_vector(d, SPLITS[d], S)
-        gather_vector(3, SPLITS[3], S)
-        gather_scalar(3, 0, BLOCK)
-        gather_scalar(3, BLOCK, 3 * BLOCK)
-        gather_scalar(3, 3 * BLOCK, SPLITS[3])
+        for d in (2, 0, 1, 3):
+            gather_vector(d, C, SPLITS[d])
+            gather_first(d, 0)
+            gather_first(d, BLOCK)
+            gather_scalar(d, SPLITS[d], S)
         quant_x(0, BLOCK)
-        quant_x(BLOCK, 3 * BLOCK)
-        quant_x(3 * BLOCK, 3 * C)
-        permute(2, nc.vector.tensor_copy)
-        quant_x(3 * C, S)
-        permute(3, nc.vector.tensor_copy)
+        quant_x(BLOCK, C)
+        weave(1, "first0")
+        quant_x(C, 2 * C)
+        for e in (2, 3):
+            weave(e, "woven%d" % e)
+            permute(e, nc.vector.tensor_copy)
+            quant_x(C * e, C * (e + 1))
         layer1(0)
         layer1(1)
         y = keep.tile([P, S], F32, name="y", align_bytes=64)

@@ -23,7 +23,8 @@ FLOPS = 2 * S * (K * H + H * N)
 BLOCK = 128
 LAYER1_BANKS = 3
 SPLITS = (832, 832, 576, 576)
-VECTOR_FIRST, SCALAR_FIRST, SCALAR_SECOND, VECTOR_SECOND = (0, 128), (128, 2 * C), (2 * C, 3 * C), (3 * C, S)
+CODE_TAGS = ("x_codes0", "x_codes1", "x_codes2", "h_raw0")
+VECTOR_FIRST, SCALAR_FIRST, VECTOR_SECOND, SCALAR_SECOND = (0, 160), (160, 2 * C), (2 * C, 3 * C), (3 * C, S)
 STORE_WIDTH = T // 3
 
 
@@ -35,7 +36,8 @@ def tile_moe_two_mlp_gelu_kernel(tc, xT, w1_words, w1_scales, w2_words, w2_scale
 
         offs_t = keep.tile([P, S // 16], U16, name="offs_t")
         dst_t = keep.tile([P, S // 16], U16, name="dst_t")
-        s1_raw = keep.tile([P, E * H], U8, name="s1_raw", align_bytes=64)
+        late = ctx.enter_context(tc.tile_pool(name="late", bufs=1))
+        s1_raw = late.tile([P, E * H], U8, name="s1_raw", align_bytes=256, offset=3 * S)
         w_scales = keep.tile([P, E * (H + N)], U8, name="w_scales", align_bytes=64)
         placed_v = keep.tile([P, T], F32, name="placed_v")
         placed_s = keep.tile([P, T], F32, name="placed_s")
@@ -79,8 +81,8 @@ def tile_moe_two_mlp_gelu_kernel(tc, xT, w1_words, w1_scales, w2_words, w2_scale
         load_w1(2, 4)
         for r in range(1, 4):
             nc.sync.dma_start(out=w_scales[r:P:32, :].bitcast(I32), in_=w_scales[8 * r : P : 32, :].bitcast(I32))
-        w2_t = keep.tile([P, E, 2 * N], U8, name="w2_t", align_bytes=64)
-        gate_t = keep.tile([P, S], F32, name="gate_t", align_bytes=64)
+        w2_t = late.tile([P, E, 2 * N], U8, name="w2_t", align_bytes=256, offset=4 * S)
+        gate_t = late.tile([P, S], F32, name="gate_t", align_bytes=256, offset=0)
         nc.sync.dma_start(out=w2_t[:].bitcast(I32), in_=w2_words[:, 0].rearrange("e p b -> p e b").bitcast(I32))
         nc.sync.dma_start(dst_t[:], dst)
         nc.sync.dma_start(out=gate_t[:], in_=gate)
@@ -121,15 +123,18 @@ def tile_moe_two_mlp_gelu_kernel(tc, xT, w1_words, w1_scales, w2_words, w2_scale
                 in_=words[:, :, C * (e - 1) : C * e].rearrange("p half s -> p s half"),
             )
 
-        x_codes = keep.tile([P, S], U32, name="x_codes", align_bytes=64)
+        x_codes = {}
         x_scales = keep.tile([P, S], U8, name="x_scales", align_bytes=64)
-        h_raw = keep.tile([P, S, 4], BF16, name="h_raw", align_bytes=64)
+        h_raw = {}
         h_codes = keep.tile([P, S], U32, name="h_codes", align_bytes=64)
         h_scales = keep.tile([P, S], U8, name="h_scales", align_bytes=64)
 
         def quant_x(s0, s1):
+            e = s0 // C
+            if e not in x_codes:
+                x_codes[e] = keep.tile([P, C], U32, name="x_codes%d" % e, align_bytes=64, tag=CODE_TAGS[e])
             nc.vector.quantize_mx(
-                out=x_codes[:, s0:s1].bitcast(FP8X4),
+                out=x_codes[e][:, s0 - C * e : s1 - C * e].bitcast(FP8X4),
                 scales=x_scales[:, s0:s1],
                 in_=woven[s0][:].rearrange("p s d -> p (s d)"),
             )
@@ -138,6 +143,7 @@ def tile_moe_two_mlp_gelu_kernel(tc, xT, w1_words, w1_scales, w2_words, w2_scale
             return "bank%d" % (s0 // BLOCK % LAYER1_BANKS)
 
         def layer1(e):
+            h_raw[e] = keep.tile([P, C, 4], BF16, name="h_raw%d" % e, align_bytes=64, tag="h_raw%d" % e)
             for a in range(0, C, BLOCK):
                 s0 = C * e + a
                 acc = psum.tile([P, 4, BLOCK], F32, name="acc", tag=block_bank(s0))
@@ -146,19 +152,19 @@ def tile_moe_two_mlp_gelu_kernel(tc, xT, w1_words, w1_scales, w2_words, w2_scale
                         out=acc[:, j, :],
                         lhsT=w1_perm[:, e, 2 * P * j : 2 * P * (j + 1)].bitcast(FP4X4),
                         lhsT_scale=w_scales[:, H * e + P * j : H * e + P * (j + 1)],
-                        rhs=x_codes[:, s0 : s0 + BLOCK].bitcast(FP8X4),
+                        rhs=x_codes[e][:, a : a + BLOCK].bitcast(FP8X4),
                         rhs_scale=x_scales[:, s0 : s0 + BLOCK],
                         start=True,
                         stop=True,
                     )
-                nc.scalar.activation(out=h_raw[:, s0 : s0 + BLOCK, :], in_=acc[:].rearrange("p j s -> p s j"), func=GELU)
+                nc.scalar.activation(out=h_raw[e][:, a : a + BLOCK, :], in_=acc[:].rearrange("p j s -> p s j"), func=GELU)
 
         def layer2(e, sums):
             slots = slice(C * e, C * (e + 1))
             nc.vector.quantize_mx(
                 out=h_codes[:, slots].bitcast(FP8X4),
                 scales=h_scales[:, slots],
-                in_=h_raw[:, slots, :].rearrange("p s j -> p (s j)"),
+                in_=h_raw[e][:].rearrange("p s j -> p (s j)"),
             )
             nc.tensor.matmul_mx(
                 out=sums,
@@ -191,7 +197,7 @@ def tile_moe_two_mlp_gelu_kernel(tc, xT, w1_words, w1_scales, w2_words, w2_scale
         for e in (2, 3):
             weave(e, "woven%d" % e)
             permute(e, nc.vector.tensor_copy)
-            quant_x(C * e, C * (e + 1))
+        quant_x(2 * C, 3 * C)
         layer1(0)
         layer1(1)
         y = keep.tile([P, S], F32, name="y", align_bytes=64)
@@ -199,6 +205,7 @@ def tile_moe_two_mlp_gelu_kernel(tc, xT, w1_words, w1_scales, w2_words, w2_scale
         sums_1 = psum.tile([P, C], F32, name="sums_1", tag="bank%d" % (LAYER1_BANKS + 2))
         sums_3 = psum.tile([P, C], F32, name="sums_3", tag="bank%d" % (LAYER1_BANKS + 1))
         layer2(0, sums_0[:])
+        quant_x(3 * C, S)
         weigh(0, 1, sums_0)
         layer1(2)
         layer2(1, sums_1[:])
@@ -212,8 +219,8 @@ def tile_moe_two_mlp_gelu_kernel(tc, xT, w1_words, w1_scales, w2_words, w2_scale
         scatter_scalar(*SCALAR_FIRST)
         weigh(2, 3, sums_2)
         weigh(3, 4, sums_3)
-        scatter_scalar(*SCALAR_SECOND)
         scatter_vector(*VECTOR_SECOND)
+        scatter_scalar(*SCALAR_SECOND)
 
         for a, queue in zip(range(0, T, STORE_WIDTH), (nc.sync, nc.scalar, nc.sync)):
             piece = slice(a, a + STORE_WIDTH)

@@ -22,9 +22,9 @@ FLOPS = 2 * S * (K * H + H * N)
 
 BLOCK = 128
 LAYER1_BANKS = 3
-SPLITS = (832, 832, 576, 576)
+SPLITS = (896, 896, 512, 512)
 CODE_TAGS = ("x_codes0", "x_codes1", "x_codes2", "h_raw0")
-VECTOR_FIRST, SCALAR_FIRST, VECTOR_SECOND, SCALAR_SECOND = (0, 160), (160, 2 * C), (2 * C, 3 * C), (3 * C, S)
+VECTOR_FIRST, SCALAR_FIRST, VECTOR_SECOND, SCALAR_SECOND = (0, 192), (192, 480), (480, 3 * C), (3 * C, S)
 STORE_WIDTH = T // 3
 
 
@@ -95,8 +95,8 @@ def tile_moe_two_mlp_gelu_kernel(tc, xT, w1_words, w1_scales, w2_words, w2_scale
                 in_=w1_raw[e].bitcast(U16).rearrange("p (m j) -> p j m", j=4),
             )
 
-        permute(0, nc.scalar.copy)
-        permute(1, nc.scalar.copy)
+        permute(0, nc.vector.tensor_copy)
+        permute(1, nc.vector.tensor_copy)
 
         woven = {}
         for block in range(C // BLOCK):

@@ -24,7 +24,7 @@ BLOCK = 128
 LAYER1_BANKS = 3
 SPLITS = (896, 896, 512, 512)
 CODE_TAGS = ("x_codes0", "x_codes1", "x_codes2", "h_raw0")
-VECTOR_FIRST, SCALAR_FIRST, VECTOR_SECOND, SCALAR_SECOND = (0, 192), (192, 480), (480, 3 * C), (3 * C, S)
+VECTOR_FIRST, SCALAR_FIRST, VECTOR_SECOND, SCALAR_SECOND = (0, 192), (192, 2 * C), (2 * C, 3 * C), (3 * C, S)
 STORE_WIDTH = T // 3
 
 
@@ -48,8 +48,6 @@ def tile_moe_two_mlp_gelu_kernel(tc, xT, w1_words, w1_scales, w2_words, w2_scale
         nc.scalar.activation(out=placed_s[:], in_=zero[:].to_broadcast([P, T]), func=GELU)
         nc.gpsimd.memset(w_scales[:, E * H :].bitcast(I32), 0)
         nc.gpsimd.memset(placed_v[:], 0.0)
-        zeros = keep.tile([P, VECTOR_FIRST[1]], F32, name="zeros")
-        nc.gpsimd.memset(zeros[:], 0.0)
 
         w1_raw = {}
 
@@ -211,8 +209,7 @@ def tile_moe_two_mlp_gelu_kernel(tc, xT, w1_words, w1_scales, w2_words, w2_scale
         layer2(1, sums_1[:])
         layer1(3)
         sums_2 = psum.tile([P, C], F32, name="sums_2", tag=block_bank(S - BLOCK))
-        s0, s1 = VECTOR_FIRST
-        nc.vector.tensor_tensor(placed_v[:].indirect(dst_t[:, s0 // 16 : s1 // 16]), y[:, s0:s1], zeros[:], ADD)
+        scatter_vector(*VECTOR_FIRST)
         weigh(1, 2, sums_1)
         layer2(2, sums_2[:])
         layer2(3, sums_3[:])

@@ -24,7 +24,7 @@ BLOCK = 128
 LAYER1_BANKS = 3
 SPLITS = (896, 896, 512, 512)
 CODE_TAGS = ("x_codes0", "x_codes1", "x_codes2", "h_raw0")
-VECTOR_FIRST, SCALAR_FIRST, VECTOR_SECOND, SCALAR_SECOND = (0, 192), (192, 2 * C), (2 * C, 3 * C), (3 * C, S)
+VECTOR_FIRST, SCALAR_FIRST, VECTOR_SECOND, SCALAR_SECOND = (0, 160), (160, 416), (416, 3 * C), (3 * C, S)
 STORE_WIDTH = T // 3
 
 
@@ -48,6 +48,8 @@ def tile_moe_two_mlp_gelu_kernel(tc, xT, w1_words, w1_scales, w2_words, w2_scale
         nc.scalar.activation(out=placed_s[:], in_=zero[:].to_broadcast([P, T]), func=GELU)
         nc.gpsimd.memset(w_scales[:, E * H :].bitcast(I32), 0)
         nc.gpsimd.memset(placed_v[:], 0.0)
+        zeros = keep.tile([P, VECTOR_FIRST[1]], F32, name="zeros")
+        nc.gpsimd.memset(zeros[:], 0.0)
 
         w1_raw = {}
 
@@ -209,7 +211,8 @@ def tile_moe_two_mlp_gelu_kernel(tc, xT, w1_words, w1_scales, w2_words, w2_scale
         layer2(1, sums_1[:])
         layer1(3)
         sums_2 = psum.tile([P, C], F32, name="sums_2", tag=block_bank(S - BLOCK))
-        scatter_vector(*VECTOR_FIRST)
+        s0, s1 = VECTOR_FIRST
+        nc.vector.tensor_tensor(placed_v[:].indirect(dst_t[:, s0 // 16 : s1 // 16]), y[:, s0:s1], zeros[:], ADD)
         weigh(1, 2, sums_1)
         layer2(2, sums_2[:])
         layer2(3, sums_3[:])

@@ -24,7 +24,7 @@ BLOCK = 128
 LAYER1_BANKS = 3
 SPLITS = (896, 896, 512, 512)
 CODE_TAGS = ("x_codes0", "x_codes1", "x_codes2", "h_raw0")
-VECTOR_FIRST, SCALAR_FIRST, VECTOR_SECOND, SCALAR_SECOND = (0, 160), (160, 416), (416, 3 * C), (3 * C, S)
+VECTOR_FIRST, SCALAR_FIRST, VECTOR_SECOND, SCALAR_SECOND = (0, 160), (160, 448), (448, 3 * C), (3 * C, S)
 STORE_WIDTH = T // 3
 
 

from contextlib import ExitStack

import concourse.mybir as mybir

F32 = mybir.dt.float32
BF16 = mybir.dt.bfloat16
I32 = mybir.dt.int32
U32 = mybir.dt.uint32
U16 = mybir.dt.uint16
U8 = mybir.dt.uint8
FP8X4 = mybir.dt.float8_e4m3fn_x4
FP4X4 = mybir.dt.float4_e2m1fn_x4
GELU = mybir.ActivationFunctionType.Gelu_apprx_tanh
COPY = mybir.ActivationFunctionType.Copy
MULT = mybir.AluOpType.mult
ADD = mybir.AluOpType.add

P = 128
K, T, E, C, H, N = 512, 1536, 4, 256, 512, 128
S = E * C
FLOPS = 2 * S * (K * H + H * N)

BLOCK = 128
LAYER1_BANKS = 3
SPLITS = (896, 896, 512, 512)
CODE_TAGS = ("x_codes0", "x_codes1", "x_codes2", "h_raw0")
VECTOR_FIRST, SCALAR_FIRST, VECTOR_SECOND, SCALAR_SECOND = (0, 160), (160, 448), (448, 3 * C), (3 * C, S)
STORE_WIDTH = T // 3


def tile_moe_two_mlp_gelu_kernel(tc, xT, w1_words, w1_scales, w2_words, w2_scales, gate, offs, dst, out):
    nc = tc.nc
    with ExitStack() as ctx:
        keep = ctx.enter_context(tc.tile_pool(name="keep", bufs=1))
        psum = ctx.enter_context(tc.psum_pool(name="psum", bufs=1))

        offs_t = keep.tile([P, S // 16], U16, name="offs_t")
        dst_t = keep.tile([P, S // 16], U16, name="dst_t")
        late = ctx.enter_context(tc.tile_pool(name="late", bufs=1))
        s1_raw = late.tile([P, E * H], U8, name="s1_raw", align_bytes=256, offset=3 * S)
        w_scales = keep.tile([P, E * (H + N)], U8, name="w_scales", align_bytes=64)
        placed_v = keep.tile([P, T], F32, name="placed_v")
        placed_s = keep.tile([P, T], F32, name="placed_s")
        zero = keep.tile([P, 1], F32, name="zero")

        nc.gpsimd.memset(zero[:], 0.0)
        nc.gpsimd.memset(s1_raw[:].bitcast(I32), 0)
        nc.scalar.activation(out=placed_s[:], in_=zero[:].to_broadcast([P, T]), func=GELU)
        nc.gpsimd.memset(w_scales[:, E * H :].bitcast(I32), 0)
        nc.gpsimd.memset(placed_v[:], 0.0)
        zeros = keep.tile([P, VECTOR_FIRST[1]], F32, name="zeros")
        nc.gpsimd.memset(zeros[:], 0.0)

        w1_raw = {}

        def load_w1(e0, e1):
            raw = keep.tile([P, e1 - e0, 2 * H], U8, name="w1_raw%d" % e0, align_bytes=256)
            nc.sync.dma_start(out=raw[:].bitcast(I32), in_=w1_words[e0:e1, 0].rearrange("e p b -> p e b").bitcast(I32))
            for e in range(e0, e1):
                w1_raw[e] = raw[:, e - e0, :]

        load_w1(0, 2)
        nc.sync.dma_start(
            out=s1_raw[0:P:8, :].rearrange("q (e i) -> q e i", e=E).bitcast(I32),
            in_=w1_scales[:, 0].rearrange("e q i -> q e i").bitcast(I32),
        )
        x_rows = xT.rearrange("(p d) t -> d p t", d=4)
        planes = [keep.tile([P, T], F32, name="plane%d" % d, align_bytes=256) for d in range(4)]
        nc.sync.dma_start(out=planes[2][:], in_=x_rows[2])
        nc.sync.dma_start(offs_t[:], offs)
        nc.sync.dma_start(
            out=w_scales[0:P:8, E * H :].rearrange("q (e n) -> q e n", e=E).bitcast(I32),
            in_=w2_scales[:, 0].rearrange("e q n -> q e n").bitcast(I32),
        )
        for d in (0, 1, 3):
            nc.sync.dma_start(out=planes[d][:], in_=x_rows[d])
        nc.vector.tensor_copy(
            out=w_scales[:, : E * H].rearrange("p (e j m) -> p e j m", e=E, j=4),
            in_=s1_raw[:].rearrange("p (e m j) -> p e j m", e=E, j=4),
        )
        load_w1(2, 4)
        for r in range(1, 4):
            nc.sync.dma_start(out=w_scales[r:P:32, :].bitcast(I32), in_=w_scales[8 * r : P : 32, :].bitcast(I32))
        w2_t = late.tile([P, E, 2 * N], U8, name="w2_t", align_bytes=256, offset=4 * S)
        gate_t = late.tile([P, S], F32, name="gate_t", align_bytes=256, offset=0)
        nc.sync.dma_start(out=w2_t[:].bitcast(I32), in_=w2_words[:, 0].rearrange("e p b -> p e b").bitcast(I32))
        nc.sync.dma_start(dst_t[:], dst)
        nc.sync.dma_start(out=gate_t[:], in_=gate)

        w1_perm = keep.tile([P, E, 2 * H], U8, name="w1_perm", align_bytes=64)

        def permute(e, engine_copy):
            engine_copy(
                out=w1_perm[:, e, :].bitcast(U16).rearrange("p (j m) -> p j m", j=4),
                in_=w1_raw[e].bitcast(U16).rearrange("p (m j) -> p j m", j=4),
            )

        permute(0, nc.vector.tensor_copy)
        permute(1, nc.vector.tensor_copy)

        woven = {}
        for block in range(C // BLOCK):
            woven[BLOCK * block] = keep.tile([P, BLOCK, 4], BF16, name="first%d" % block, align_bytes=64, tag="first%d" % block)
        pairs = keep.tile([P, 2, S - C, 2], BF16, name="pairs", align_bytes=64)

        def picked(d, s0, s1):
            return planes[d][:].indirect(offs_t[:, s0 // 16 : s1 // 16])

        def gather_vector(d, s0, s1):
            nc.vector.tensor_copy(out=pairs[:, d // 2, s0 - C : s1 - C, d % 2], in_=picked(d, s0, s1))

        def gather_scalar(d, s0, s1):
            nc.scalar.activation(out=pairs[:, d // 2, s0 - C : s1 - C, d % 2], in_=picked(d, s0, s1), func=COPY)

        def gather_first(d, s0):
            nc.scalar.activation(out=woven[s0][:, :, d], in_=picked(d, s0, s0 + BLOCK), func=COPY)

        def weave(e, tag):
            woven[C * e] = keep.tile([P, C, 4], BF16, name="woven%d" % e, align_bytes=64, tag=tag)
            words = pairs[:].rearrange("p half s j -> p half (s j)").bitcast(I32)
            nc.vector.tensor_copy(
                out=woven[C * e][:].rearrange("p s d -> p (s d)").bitcast(I32).rearrange("p (s half) -> p s half", half=2),
                in_=words[:, :, C * (e - 1) : C * e].rearrange("p half s -> p s half"),
            )

        x_codes = {}
        x_scales = keep.tile([P, S], U8, name="x_scales", align_bytes=64)
        h_raw = {}
        h_codes = keep.tile([P, S], U32, name="h_codes", align_bytes=64)
        h_scales = keep.tile([P, S], U8, name="h_scales", align_bytes=64)

        def quant_x(s0, s1):
            e = s0 // C
            if e not in x_codes:
                x_codes[e] = keep.tile([P, C], U32, name="x_codes%d" % e, align_bytes=64, tag=CODE_TAGS[e])
            nc.vector.quantize_mx(
                out=x_codes[e][:, s0 - C * e : s1 - C * e].bitcast(FP8X4),
                scales=x_scales[:, s0:s1],
                in_=woven[s0][:].rearrange("p s d -> p (s d)"),
            )

        def block_bank(s0):
            return "bank%d" % (s0 // BLOCK % LAYER1_BANKS)

        def layer1(e):
            h_raw[e] = keep.tile([P, C, 4], BF16, name="h_raw%d" % e, align_bytes=64, tag="h_raw%d" % e)
            for a in range(0, C, BLOCK):
                s0 = C * e + a
                acc = psum.tile([P, 4, BLOCK], F32, name="acc", tag=block_bank(s0))
                for j in range(4):
                    nc.tensor.matmul_mx(
                        out=acc[:, j, :],
                        lhsT=w1_perm[:, e, 2 * P * j : 2 * P * (j + 1)].bitcast(FP4X4),
                        lhsT_scale=w_scales[:, H * e + P * j : H * e + P * (j + 1)],
                        rhs=x_codes[e][:, a : a + BLOCK].bitcast(FP8X4),
                        rhs_scale=x_scales[:, s0 : s0 + BLOCK],
                        start=True,
                        stop=True,
                    )
                nc.scalar.activation(out=h_raw[e][:, a : a + BLOCK, :], in_=acc[:].rearrange("p j s -> p s j"), func=GELU)

        def layer2(e, sums):
            slots = slice(C * e, C * (e + 1))
            nc.vector.quantize_mx(
                out=h_codes[:, slots].bitcast(FP8X4),
                scales=h_scales[:, slots],
                in_=h_raw[e][:].rearrange("p s j -> p (s j)"),
            )
            nc.tensor.matmul_mx(
                out=sums,
                lhsT=w2_t[:, e, :].bitcast(FP4X4),
                lhsT_scale=w_scales[:, E * H + N * e : E * H + N * (e + 1)],
                rhs=h_codes[:, slots].bitcast(FP8X4),
                rhs_scale=h_scales[:, slots],
                start=True,
                stop=True,
            )

        def weigh(e0, e1, sums):
            nc.vector.tensor_tensor(y[:, C * e0 : C * e1], sums[:], gate_t[:, C * e0 : C * e1], MULT)

        def scatter_vector(s0, s1):
            nc.vector.tensor_copy(placed_v[:].indirect(dst_t[:, s0 // 16 : s1 // 16]), y[:, s0:s1])

        def scatter_scalar(s0, s1):
            nc.scalar.activation(placed_s[:].indirect(dst_t[:, s0 // 16 : s1 // 16]), y[:, s0:s1], COPY)

        for d in (2, 0, 1, 3):
            gather_vector(d, C, SPLITS[d])
            gather_first(d, 0)
            gather_first(d, BLOCK)
            gather_scalar(d, SPLITS[d], S)
        quant_x(0, BLOCK)
        quant_x(BLOCK, C)
        weave(1, "first0")
        quant_x(C, 2 * C)
        for e in (2, 3):
            weave(e, "woven%d" % e)
            permute(e, nc.vector.tensor_copy)
        quant_x(2 * C, 3 * C)
        layer1(0)
        layer1(1)
        y = keep.tile([P, S], F32, name="y", align_bytes=64)
        sums_0 = psum.tile([P, C], F32, name="sums_0", tag="bank%d" % LAYER1_BANKS)
        sums_1 = psum.tile([P, C], F32, name="sums_1", tag="bank%d" % (LAYER1_BANKS + 2))
        sums_3 = psum.tile([P, C], F32, name="sums_3", tag="bank%d" % (LAYER1_BANKS + 1))
        layer2(0, sums_0[:])
        quant_x(3 * C, S)
        weigh(0, 1, sums_0)
        layer1(2)
        layer2(1, sums_1[:])
        layer1(3)
        sums_2 = psum.tile([P, C], F32, name="sums_2", tag=block_bank(S - BLOCK))
        s0, s1 = VECTOR_FIRST
        nc.vector.tensor_tensor(placed_v[:].indirect(dst_t[:, s0 // 16 : s1 // 16]), y[:, s0:s1], zeros[:], ADD)
        weigh(1, 2, sums_1)
        layer2(2, sums_2[:])
        layer2(3, sums_3[:])
        scatter_scalar(*SCALAR_FIRST)
        weigh(2, 3, sums_2)
        weigh(3, 4, sums_3)
        scatter_vector(*VECTOR_SECOND)
        scatter_scalar(*SCALAR_SECOND)

        for a, queue in zip(range(0, T, STORE_WIDTH), (nc.sync, nc.scalar, nc.sync)):
            piece = slice(a, a + STORE_WIDTH)
            nc.vector.tensor_tensor(placed_v[:, piece], placed_v[:, piece], placed_s[:, piece], ADD)
            queue.dma_start(out=out[:, piece], in_=placed_v[:, piece])
